import numpy as np
import ml_dtypes


def mxq(x, axis, fmt="e4m3"):
    dtype, down = {"e4m3": (ml_dtypes.float8_e4m3fn, 7), "e5m2": (ml_dtypes.float8_e5m2, 14)}[fmt]
    v = np.moveaxis(np.asarray(x, np.float32).astype(ml_dtypes.bfloat16).astype(np.float64), axis, -1)
    blocks = v.reshape(v.shape[:-1] + (-1, 32))
    amax = np.abs(blocks).max(-1, keepdims=True)
    byte = np.maximum(np.where(amax > 0, np.frexp(amax)[1] - 1 + 127, 0) - down, 1)
    scale = np.exp2(byte - 127.0)
    codes = (blocks / scale).astype(np.float32).astype(dtype).astype(np.float64)
    return np.moveaxis((codes * scale).reshape(v.shape), -1, axis)


WIDE = False


def mx_kscale(k):
    if not WIDE:
        return np.ones(k)
    levels = np.array([10, -10, 5, -5, 0])
    if k % 512:
        return np.exp2(np.random.permutation(np.resize(levels, k // 32))).repeat(32)
    a = np.empty((k // 512, 16))
    for p in range(k // 512):
        a[p, :8] = np.random.permutation(np.resize(levels, 8))
        for g in range(8):
            far = levels[np.abs(levels - a[p, g]) >= 10]
            a[p, g + 8] = far[np.random.randint(len(far))]
    return np.exp2(a.ravel()).repeat(32)


def f64(x):
    return np.asarray(x).astype(np.float64)


def striped(idx):
    return np.tile(idx.reshape(-1, 16).T, (8, 1)).astype(np.uint16)


def unstriped(offs):
    return offs[:16].T.reshape(-1).astype(np.int64)


E2M1 = np.array([0.0, 0.5, 1.0, 1.5, 2.0, 3.0, 4.0, 6.0, -0.0, -0.5, -1.0, -1.5, -2.0, -3.0, -4.0, -6.0])


def pack_weight(w, fmt):
    k, n = w.shape
    w = f64(np.asarray(w, np.float32).astype(ml_dtypes.bfloat16)).reshape(k // 32, 32, n)
    amax = np.abs(w).max(1)
    if fmt == "e4m3":
        byte = np.frexp(amax)[1] - 1 + 127 - 7
    else:
        mant, ex = np.frexp(amax / 6.0)
        byte = np.where(mant > 0.5, ex, ex - 1) + 127
    byte = np.clip(np.where(amax > 0, byte, 1), 1, 254)
    scaled = (w * np.exp2(127.0 - byte)[:, None, :]).reshape(k, n).astype(np.float32)
    by_word = np.ascontiguousarray(scaled.reshape(k // 512, 128, 4, n).transpose(0, 1, 3, 2))
    if fmt == "e4m3":
        words = by_word.astype(ml_dtypes.float8_e4m3fn).view(np.uint8)
    else:
        c = by_word.astype(ml_dtypes.float4_e2m1fn).view(np.uint8) & 0xF
        words = (c[..., 0::2] | (c[..., 1::2] << 4)).reshape(k // 512, 128, 2 * n)
    return np.ascontiguousarray(words), np.ascontiguousarray(byte.astype(np.uint8).reshape(k // 512, 16, n))


def unpack_weight(words, scales, fmt):
    g, _, n = scales.shape
    words = np.ascontiguousarray(words).reshape(g, 128, n, -1)
    if fmt == "e4m3":
        vals = words.view(ml_dtypes.float8_e4m3fn).astype(np.float64)
    else:
        nib = np.empty((g, 128, n, 4), np.uint8)
        nib[..., 0::2] = words & 0xF
        nib[..., 1::2] = words >> 4
        vals = E2M1[nib]
    vals = vals * np.repeat(np.exp2(scales.astype(np.float64) - 127.0), 8, axis=1)[..., None]
    return vals.transpose(0, 1, 3, 2).reshape(g * 512, n)


def split(x):
    m, e = np.frexp(f64(x))
    hi = np.ldexp(np.trunc(16.0 * m) / 16.0, e)
    return hi, f64(x) - hi


K, M, T, S = 1024, 256, 4096, 2048


def setup_inputs():
    n = np.random.standard_normal
    s = mx_kscale(K)[:, None]
    v = pack_weight(n((K, T)) * s, "e4m3")
    return {
        "tab_words": v[0],
        "tab_scales": v[1],
        "w": (n((K, M)) / np.sqrt(K) / s).astype(np.float32),
        "gT": n((M, T)).astype(np.float32),
        "b": (0.3 * n(256)).astype(np.float32),
        "offs": striped(np.random.permutation(T)[:S]),
    }


def reference(tab_words, tab_scales, w, gT, b, offs):
    tab_ = unpack_weight(tab_words, tab_scales, "e4m3")[:, unstriped(offs)]
    w_hi, w_lo = split(w)
    w_hi_, w_lo_ = mxq(w_hi, 0, "e4m3"), mxq(w_lo, 0, "e4m3")
    y = w_hi_.T @ tab_ + w_lo_.T @ tab_
    return (y + f64(b)[:, None]) * f64(gT)[:, unstriped(offs)]

@@ -1,0 +1,117 @@
+from contextlib import ExitStack
+
+import concourse.mybir as mybir
+
+K, M, T, S = 1024, 256, 4096, 2048
+FLOPS = 2 * 2 * K * M * S
+
+F32 = mybir.dt.float32
+BF16 = mybir.dt.bfloat16
+I32 = mybir.dt.int32
+U32 = mybir.dt.uint32
+U16 = mybir.dt.uint16
+U8 = mybir.dt.uint8
+FP8X4 = mybir.dt.float8_e4m3fn_x4
+ALU = mybir.AluOpType
+IDENTITY = mybir.ActivationFunctionType.Identity
+
+P = 128
+PACK = 4
+K_PASS = P * PACK
+PASSES = K // K_PASS
+N_TILES = M // P
+BANK = 512
+CHUNKS = S // BANK
+GROUP = 16
+HI_MASK = -(1 << 20)
+GATE_PIECES = ((1024, 1024), (1024, 512, 256, 128, 128))
+
+
+def tile_list_tabgate_bias_kernel(tc, tab_words, tab_scales, w, gT, b, offs, out):
+    nc = tc.nc
+    with ExitStack() as ctx:
+        keep = ctx.enter_context(tc.tile_pool(name="keep", bufs=1))
+        psum = ctx.enter_context(tc.psum_pool(name="psum", bufs=1))
+
+        offsets = keep.tile([P, S // GROUP], U16, name="offsets")
+        w_raw = [keep.tile([P, PACK, M], F32, name="w_raw%d" % a, align_bytes=64) for a in range(PASSES)]
+        scale_table = keep.tile([P, T // 4], I32, name="scale_table", align_bytes=64)
+        word_table = [keep.tile([P, T], I32, name="word_table%d" % a, align_bytes=64) for a in range(PASSES)]
+        gate_table = [keep.tile([P, T], F32, name="gate_table%d" % n, align_bytes=64) for n in range(N_TILES)]
+        bias = keep.tile([P, N_TILES], F32, name="bias")
+
+        nc.vector.memset(scale_table[:], 0)
+        for a in range(PASSES):
+            nc.sync.dma_start(out=w_raw[a][:], in_=w[a * K_PASS : (a + 1) * K_PASS, :].rearrange("(p j) n -> p j n", j=PACK))
+        nc.sync.dma_start(offsets[:], offs)
+        for q in range(4):
+            nc.sync.dma_start(out=scale_table[32 * q : 32 * q + 4 * PASSES, :], in_=tab_scales[:, 4 * q : 4 * q + 4, :].bitcast(I32))
+        for a in range(PASSES):
+            nc.sync.dma_start(out=word_table[a][:], in_=tab_words[a].rearrange("p t i -> p (t i)").bitcast(I32))
+        with nc.allow_non_contiguous_dma(reason="one bias value a partition"):
+            nc.sync.dma_start(out=bias[:], in_=b.rearrange("(c p) -> p c", p=P))
+        for n in range(N_TILES):
+            nc.sync.dma_start(out=gate_table[n][:], in_=gT[n * P : (n + 1) * P, :])
+
+        hi_bits = [keep.tile([P, PACK, M], I32, name="hi_bits%d" % a, align_bytes=64) for a in range(PASSES)]
+        hi_bf = keep.tile([P, PASSES, M, PACK], BF16, name="hi_bf", align_bytes=64)
+        lo_bf = keep.tile([P, PASSES, M, PACK], BF16, name="lo_bf", align_bytes=64)
+
+        def rows(ap):
+            return ap.rearrange("p j (c i) -> p c j i", i=4)
+
+        def packed(ap):
+            return ap.rearrange("p (c i) j -> p c j i", i=4)
+
+        for a in range(PASSES):
+            nc.vector.tensor_scalar(out=hi_bits[a][:], in0=w_raw[a][:].bitcast(I32), scalar1=HI_MASK, scalar2=None, op0=ALU.bitwise_and)
+        for a in range(PASSES):
+            nc.scalar.activation(out=packed(hi_bf[:, a]), in_=rows(hi_bits[a][:].bitcast(F32)), func=IDENTITY)
+            nc.vector.tensor_tensor(out=packed(lo_bf[:, a]), in0=rows(w_raw[a][:]), in1=rows(hi_bits[a][:].bitcast(F32)), op=ALU.subtract)
+
+        w_codes = [keep.tile([P, PASSES * M], U32, name="w_codes%d" % h, align_bytes=64) for h in range(2)]
+        w_scales = [keep.tile([P, PASSES * M], U8, name="w_scales%d" % h, align_bytes=64) for h in range(2)]
+        for h, part in enumerate((hi_bf, lo_bf)):
+            nc.vector.quantize_mx(out=w_codes[h][:].bitcast(FP8X4), scales=w_scales[h][:], in_=part[:].rearrange("p a n j -> p (a n j)"))
+
+        def picks(first, count):
+            return offsets[:, first // GROUP : (first + count) // GROUP]
+
+        v_scales = keep.tile([P, S], U8, name="v_scales", align_bytes=64)
+        nc.vector.tensor_copy(out=v_scales[:], in_=scale_table[:].bitcast(U8).indirect(offsets[:]))
+        v_words = [keep.tile([P, S], U32, name="v_words%d" % a, align_bytes=64) for a in range(PASSES)]
+        acc = [[psum.tile([P, BANK], F32, name="acc%d_%d" % (n, c)) for c in range(CHUNKS)] for n in range(N_TILES)]
+        y = [keep.tile([P, S], F32, name="y%d" % n, align_bytes=64) for n in range(N_TILES)]
+
+        def passes(a, n, c):
+            cols = slice(c * BANK, (c + 1) * BANK)
+            w_cols = slice(a * M + n * P, a * M + (n + 1) * P)
+            for h in range(2):
+                nc.tensor.matmul_mx(
+                    out=acc[n][c][:],
+                    lhsT=w_codes[h][:, w_cols].bitcast(FP8X4),
+                    lhsT_scale=w_scales[h][:, w_cols],
+                    rhs=v_words[a][:, cols].bitcast(FP8X4),
+                    rhs_scale=v_scales[4 * a : P, cols],
+                    start=(a == 0 and h == 0),
+                    stop=(a == PASSES - 1 and h == 1),
+                )
+
+        nc.vector.tensor_copy(out=v_words[0][:], in_=word_table[0][:].bitcast(U32).indirect(offsets[:]))
+        for n in range(N_TILES):
+            for c in range(CHUNKS):
+                passes(0, n, c)
+        for c in range(CHUNKS):
+            cols = slice(c * BANK, (c + 1) * BANK)
+            nc.vector.tensor_copy(out=v_words[1][:, cols], in_=word_table[1][:].bitcast(U32).indirect(picks(c * BANK, BANK)))
+            for n in range(N_TILES):
+                passes(1, n, c)
+                nc.scalar.activation(out=y[n][:, cols], in_=acc[n][c][:], func=IDENTITY, bias=bias[:, n : n + 1])
+
+        for n in range(N_TILES):
+            first = 0
+            for count in GATE_PIECES[n]:
+                gated = keep.tile([P, count], F32, name="gated%d_%d" % (n, first), align_bytes=64)
+                nc.vector.tensor_tensor(out=gated[:], in0=gate_table[n][:].indirect(picks(first, count)), in1=y[n][:, first : first + count], op=ALU.mult)
+                nc.sync.dma_start(out=out[n * P : (n + 1) * P, first : first + count], in_=gated[:])
+                first += count

@@ -97,16 +97,19 @@ def tile_list_tabgate_bias_kernel(tc, tab_words, tab_scales, w, gT, b, offs, out
                     stop=(a == PASSES - 1 and h == 1),
                 )
 
-        nc.vector.tensor_copy(out=v_words[0][:], in_=word_table[0][:].bitcast(U32).indirect(offsets[:]))
-        for n in range(N_TILES):
+        def add_bias(n, c):
+            nc.scalar.activation(out=y[n][:, c * BANK : (c + 1) * BANK], in_=acc[n][c][:], func=IDENTITY, bias=bias[:, n : n + 1])
+
+        for a in range(PASSES):
             for c in range(CHUNKS):
-                passes(0, n, c)
+                nc.vector.tensor_copy(out=v_words[a][:, c * BANK : (c + 1) * BANK], in_=word_table[a][:].bitcast(U32).indirect(picks(c * BANK, BANK)))
+                passes(a, 0, c)
+                if a == PASSES - 1:
+                    add_bias(0, c)
         for c in range(CHUNKS):
-            cols = slice(c * BANK, (c + 1) * BANK)
-            nc.vector.tensor_copy(out=v_words[1][:, cols], in_=word_table[1][:].bitcast(U32).indirect(picks(c * BANK, BANK)))
-            for n in range(N_TILES):
-                passes(1, n, c)
-                nc.scalar.activation(out=y[n][:, cols], in_=acc[n][c][:], func=IDENTITY, bias=bias[:, n : n + 1])
+            for a in range(PASSES):
+                passes(a, 1, c)
+            add_bias(1, c)
 
         for n in range(N_TILES):
             first = 0

@@ -40,12 +40,15 @@ def tile_list_tabgate_bias_kernel(tc, tab_words, tab_scales, w, gT, b, offs, out
         gate_table = [keep.tile([P, T], F32, name="gate_table%d" % n, align_bytes=64) for n in range(N_TILES)]
         bias = keep.tile([P, N_TILES], F32, name="bias")
 
-        nc.vector.memset(scale_table[:], 0)
-        for a in range(PASSES):
+        def load_w(a):
             nc.sync.dma_start(out=w_raw[a][:], in_=w[a * K_PASS : (a + 1) * K_PASS, :].rearrange("(p j) n -> p j n", j=PACK))
+
+        nc.vector.memset(scale_table[:], 0)
+        load_w(0)
         nc.sync.dma_start(offsets[:], offs)
         for q in range(4):
             nc.sync.dma_start(out=scale_table[32 * q : 32 * q + 4 * PASSES, :], in_=tab_scales[:, 4 * q : 4 * q + 4, :].bitcast(I32))
+        load_w(1)
         for a in range(PASSES):
             nc.sync.dma_start(out=word_table[a][:], in_=tab_words[a].rearrange("p t i -> p (t i)").bitcast(I32))
         with nc.allow_non_contiguous_dma(reason="one bias value a partition"):
@@ -53,44 +56,37 @@ def tile_list_tabgate_bias_kernel(tc, tab_words, tab_scales, w, gT, b, offs, out
         for n in range(N_TILES):
             nc.sync.dma_start(out=gate_table[n][:], in_=gT[n * P : (n + 1) * P, :])
 
-        hi_bits = [keep.tile([P, PACK, M], I32, name="hi_bits%d" % a, align_bytes=64) for a in range(PASSES)]
-        hi_bf = keep.tile([P, PASSES, M, PACK], BF16, name="hi_bf", align_bytes=64)
-        lo_bf = keep.tile([P, PASSES, M, PACK], BF16, name="lo_bf", align_bytes=64)
-
-        def rows(ap):
-            return ap.rearrange("p j (c i) -> p c j i", i=4)
-
-        def packed(ap):
-            return ap.rearrange("p (c i) j -> p c j i", i=4)
-
-        for a in range(PASSES):
-            nc.vector.tensor_scalar(out=hi_bits[a][:], in0=w_raw[a][:].bitcast(I32), scalar1=HI_MASK, scalar2=None, op0=ALU.bitwise_and)
-        for a in range(PASSES):
-            nc.scalar.activation(out=packed(hi_bf[:, a]), in_=rows(hi_bits[a][:].bitcast(F32)), func=IDENTITY)
-            nc.vector.tensor_tensor(out=packed(lo_bf[:, a]), in0=rows(w_raw[a][:]), in1=rows(hi_bits[a][:].bitcast(F32)), op=ALU.subtract)
-
-        w_codes = [keep.tile([P, PASSES * M], U32, name="w_codes%d" % h, align_bytes=64) for h in range(2)]
-        w_scales = [keep.tile([P, PASSES * M], U8, name="w_scales%d" % h, align_bytes=64) for h in range(2)]
-        for h, part in enumerate((hi_bf, lo_bf)):
-            nc.vector.quantize_mx(out=w_codes[h][:].bitcast(FP8X4), scales=w_scales[h][:], in_=part[:].rearrange("p a n j -> p (a n j)"))
-
         def picks(first, count):
             return offsets[:, first // GROUP : (first + count) // GROUP]
 
+        w_codes = [keep.tile([P, 2 * M], U32, name="w_codes%d" % a, align_bytes=64) for a in range(PASSES)]
+        w_scales = [keep.tile([P, 2 * M], U8, name="w_scales%d" % a, align_bytes=64) for a in range(PASSES)]
+        w_split = [keep.tile([P, 2, M, PACK], BF16, name="w_split%d" % a, align_bytes=64) for a in range(PASSES)]
         v_scales = keep.tile([P, S], U8, name="v_scales", align_bytes=64)
-        nc.vector.tensor_copy(out=v_scales[:], in_=scale_table[:].bitcast(U8).indirect(offsets[:]))
+        for a in range(PASSES):
+            hi_bits = keep.tile([P, PACK, M], I32, name="hi_bits%d" % a, align_bytes=64)
+            lo_rows = keep.tile([P, PACK, M], F32, name="lo_rows%d" % a, align_bytes=64)
+            nc.vector.tensor_scalar(out=hi_bits[:], in0=w_raw[a][:].bitcast(I32), scalar1=HI_MASK, scalar2=None, op0=ALU.bitwise_and)
+            nc.gpsimd.tensor_tensor(out=lo_rows[:], in0=w_raw[a][:], in1=hi_bits[:].bitcast(F32), op=ALU.subtract)
+            for h, rows in enumerate((hi_bits[:].bitcast(F32), lo_rows[:])):
+                nc.scalar.activation(out=w_split[a][:, h], in_=rows.rearrange("p j n -> p n j"), func=IDENTITY)
+            half = S // PASSES
+            nc.vector.tensor_copy(out=v_scales[:, a * half : (a + 1) * half], in_=scale_table[:].bitcast(U8).indirect(picks(a * half, half)))
+        for a in range(PASSES):
+            nc.vector.quantize_mx(out=w_codes[a][:].bitcast(FP8X4), scales=w_scales[a][:], in_=w_split[a][:].rearrange("p h n j -> p (h n j)"))
+
         v_words = [keep.tile([P, S], U32, name="v_words%d" % a, align_bytes=64) for a in range(PASSES)]
         acc = [[psum.tile([P, BANK], F32, name="acc%d_%d" % (n, c)) for c in range(CHUNKS)] for n in range(N_TILES)]
         y = [keep.tile([P, S], F32, name="y%d" % n, align_bytes=64) for n in range(N_TILES)]
 
         def passes(a, n, c):
             cols = slice(c * BANK, (c + 1) * BANK)
-            w_cols = slice(a * M + n * P, a * M + (n + 1) * P)
             for h in range(2):
+                w_cols = slice(h * M + n * P, h * M + (n + 1) * P)
                 nc.tensor.matmul_mx(
                     out=acc[n][c][:],
-                    lhsT=w_codes[h][:, w_cols].bitcast(FP8X4),
-                    lhsT_scale=w_scales[h][:, w_cols],
+                    lhsT=w_codes[a][:, w_cols].bitcast(FP8X4),
+                    lhsT_scale=w_scales[a][:, w_cols],
                     rhs=v_words[a][:, cols].bitcast(FP8X4),
                     rhs_scale=v_scales[4 * a : P, cols],
                     start=(a == 0 and h == 0),

@@ -1,6 +1,7 @@
 from contextlib import ExitStack
 
 import concourse.mybir as mybir
+from concourse.masks import make_identity
 
 K, M, T, S = 1024, 256, 4096, 2048
 FLOPS = 2 * 2 * K * M * S
@@ -24,7 +25,9 @@ BANK = 512
 CHUNKS = S // BANK
 GROUP = 16
 HI_MASK = -(1 << 20)
-GATE_PIECES = ((1024, 1024), (1024, 512, 256, 128, 128))
+SIGN_BIT = -(1 << 31)
+WORD_PIECES = ((512, 512, 1024), (512, 512, 512, 512))
+GATE_PIECES = ((1024, 1024), (1024, 512, 384, 128))
 
 
 def tile_list_tabgate_bias_kernel(tc, tab_words, tab_scales, w, gT, b, offs, out):
@@ -35,8 +38,8 @@ def tile_list_tabgate_bias_kernel(tc, tab_words, tab_scales, w, gT, b, offs, out
 
         offsets = keep.tile([P, S // GROUP], U16, name="offsets")
         w_raw = [keep.tile([P, PACK, M], F32, name="w_raw%d" % a, align_bytes=64) for a in range(PASSES)]
-        scale_table = keep.tile([P, T // 4], I32, name="scale_table", align_bytes=64)
-        word_table = [keep.tile([P, T], I32, name="word_table%d" % a, align_bytes=64) for a in range(PASSES)]
+        scale_table = keep.tile([P, T // 4], I32, name="scale_table", tag="scale_table", align_bytes=64)
+        word_table = [keep.tile([P, T], I32, name="word_table%d" % a, tag="word_table%d" % a, align_bytes=64) for a in range(PASSES)]
         gate_table = [keep.tile([P, T], F32, name="gate_table%d" % n, align_bytes=64) for n in range(N_TILES)]
         bias = keep.tile([P, N_TILES], F32, name="bias")
 
@@ -44,10 +47,11 @@ def tile_list_tabgate_bias_kernel(tc, tab_words, tab_scales, w, gT, b, offs, out
             nc.sync.dma_start(out=w_raw[a][:], in_=w[a * K_PASS : (a + 1) * K_PASS, :].rearrange("(p j) n -> p j n", j=PACK))
 
         nc.vector.memset(scale_table[:], 0)
-        load_w(0)
         nc.sync.dma_start(offsets[:], offs)
-        for q in range(4):
-            nc.sync.dma_start(out=scale_table[32 * q : 32 * q + 4 * PASSES, :], in_=tab_scales[:, 4 * q : 4 * q + 4, :].bitcast(I32))
+        load_w(0)
+        for r in range(4):
+            for a in range(PASSES):
+                nc.sync.dma_start(out=scale_table[4 * a + r : P : 32, :], in_=tab_scales[a].rearrange("(q r) t -> r q t", r=4)[r].bitcast(I32))
         load_w(1)
         for a in range(PASSES):
             nc.sync.dma_start(out=word_table[a][:], in_=tab_words[a].rearrange("p t i -> p (t i)").bitcast(I32))
@@ -56,27 +60,51 @@ def tile_list_tabgate_bias_kernel(tc, tab_words, tab_scales, w, gT, b, offs, out
         for n in range(N_TILES):
             nc.sync.dma_start(out=gate_table[n][:], in_=gT[n * P : (n + 1) * P, :])
 
+        identity = keep.tile([P, P], F32, name="identity", align_bytes=64)
+        make_identity(nc, identity[:])
+
+        def bank(index, name):
+            return psum.tile([P, BANK], F32, name=name, tag="bank%d" % index)
+
+        w_split = [keep.tile([P, 2, M, PACK], BF16, name="w_split%d" % a, align_bytes=64) for a in range(PASSES)]
+        neg_hi = [keep.tile([P, PACK, M], I32, name="neg_hi%d" % a, align_bytes=64) for a in range(PASSES)]
+
         def picks(first, count):
             return offsets[:, first // GROUP : (first + count) // GROUP]
 
-        w_codes = [keep.tile([P, 2 * M], U32, name="w_codes%d" % a, align_bytes=64) for a in range(PASSES)]
-        w_scales = [keep.tile([P, 2 * M], U8, name="w_scales%d" % a, align_bytes=64) for a in range(PASSES)]
-        w_split = [keep.tile([P, 2, M, PACK], BF16, name="w_split%d" % a, align_bytes=64) for a in range(PASSES)]
         v_scales = keep.tile([P, S], U8, name="v_scales", align_bytes=64)
+        half = S // PASSES
         for a in range(PASSES):
-            hi_bits = keep.tile([P, PACK, M], I32, name="hi_bits%d" % a, align_bytes=64)
-            lo_rows = keep.tile([P, PACK, M], F32, name="lo_rows%d" % a, align_bytes=64)
-            nc.vector.tensor_scalar(out=hi_bits[:], in0=w_raw[a][:].bitcast(I32), scalar1=HI_MASK, scalar2=None, op0=ALU.bitwise_and)
-            nc.gpsimd.tensor_tensor(out=lo_rows[:], in0=w_raw[a][:], in1=hi_bits[:].bitcast(F32), op=ALU.subtract)
-            for h, rows in enumerate((hi_bits[:].bitcast(F32), lo_rows[:])):
-                nc.scalar.activation(out=w_split[a][:, h], in_=rows.rearrange("p j n -> p n j"), func=IDENTITY)
-            half = S // PASSES
+            nc.vector.tensor_scalar(out=neg_hi[a][:], in0=w_raw[a][:].bitcast(I32), scalar1=HI_MASK, scalar2=SIGN_BIT, op0=ALU.bitwise_and, op1=ALU.bitwise_xor)
             nc.vector.tensor_copy(out=v_scales[:, a * half : (a + 1) * half], in_=scale_table[:].bitcast(U8).indirect(picks(a * half, half)))
         for a in range(PASSES):
-            nc.vector.quantize_mx(out=w_codes[a][:].bitcast(FP8X4), scales=w_scales[a][:], in_=w_split[a][:].rearrange("p h n j -> p (h n j)"))
+            lo_t = keep.tile([P, N_TILES, 2, P, 2], BF16, name="lo_t%d" % a, align_bytes=64)
+            for n in range(N_TILES):
+                diff = bank(CHUNKS + a * N_TILES + n, "diff%d_%d" % (a, n))
+                for j in range(PACK):
+                    for first, rows in ((True, w_raw[a][:]), (False, neg_hi[a][:].bitcast(F32))):
+                        nc.tensor.matmul(diff[:, j * P : (j + 1) * P], lhsT=rows[:, j, n * P : (n + 1) * P], rhs=identity[:], is_transpose=True, start=first, stop=not first)
+                nc.scalar.activation(out=lo_t[:, n], in_=diff[:].rearrange("n (u e p) -> n u p e", u=2, e=2), func=IDENTITY)
+            nc.scalar.activation(
+                out=w_split[a][:, 0].rearrange("p (c i) j -> p c j i", i=4),
+                in_=neg_hi[a][:].bitcast(F32).rearrange("p j (c i) -> p c j i", i=4),
+                func=IDENTITY,
+                scale=-1.0,
+            )
+            back = bank(CHUNKS - PASSES + a, "back%d" % a)
+            lo_words = lo_t[:].rearrange("n t u p e -> n (t u p e)").bitcast(F32)
+            for block in range(N_TILES * 2):
+                nc.tensor.transpose(back[:, block * P : (block + 1) * P], lo_words[:, block * P : (block + 1) * P], identity[:])
+            nc.scalar.copy(
+                out=w_split[a][:, 1].rearrange("p n j -> p (n j)").bitcast(F32).rearrange("p (t n u) -> p t n u", t=N_TILES, u=2),
+                in_=back[:].rearrange("p (t u n) -> p t n u", t=N_TILES, u=2),
+            )
+
+        w_scales = [keep.tile([P, 2 * M], U8, name="w_scales%d" % a, align_bytes=64) for a in range(PASSES)]
+        w_codes = []
 
         v_words = [keep.tile([P, S], U32, name="v_words%d" % a, align_bytes=64) for a in range(PASSES)]
-        acc = [[psum.tile([P, BANK], F32, name="acc%d_%d" % (n, c)) for c in range(CHUNKS)] for n in range(N_TILES)]
+        acc = [[bank(n * CHUNKS + c, "acc%d_%d" % (n, c)) for c in range(CHUNKS)] for n in range(N_TILES)]
         y = [keep.tile([P, S], F32, name="y%d" % n, align_bytes=64) for n in range(N_TILES)]
 
         def passes(a, n, c):
@@ -97,11 +125,17 @@ def tile_list_tabgate_bias_kernel(tc, tab_words, tab_scales, w, gT, b, offs, out
             nc.scalar.activation(out=y[n][:, c * BANK : (c + 1) * BANK], in_=acc[n][c][:], func=IDENTITY, bias=bias[:, n : n + 1])
 
         for a in range(PASSES):
-            for c in range(CHUNKS):
-                nc.vector.tensor_copy(out=v_words[a][:, c * BANK : (c + 1) * BANK], in_=word_table[a][:].bitcast(U32).indirect(picks(c * BANK, BANK)))
-                passes(a, 0, c)
-                if a == PASSES - 1:
-                    add_bias(0, c)
+            codes = keep.tile([P, 2 * M], U32, name="w_codes%d" % a, tag=("scale_table", "word_table0")[a], align_bytes=64)
+            nc.vector.quantize_mx(out=codes[:].bitcast(FP8X4), scales=w_scales[a][:], in_=w_split[a][:].rearrange("p h n j -> p (h n j)"))
+            w_codes.append(codes)
+            first = 0
+            for count in WORD_PIECES[a]:
+                nc.vector.tensor_copy(out=v_words[a][:, first : first + count], in_=word_table[a][:].bitcast(U32).indirect(picks(first, count)))
+                for c in range(first // BANK, (first + count) // BANK):
+                    passes(a, 0, c)
+                    if a == PASSES - 1:
+                        add_bias(0, c)
+                first += count
         for c in range(CHUNKS):
             for a in range(PASSES):
                 passes(a, 1, c)

@@ -24,6 +24,7 @@ N_TILES = M // P
 BANK = 512
 CHUNKS = S // BANK
 GROUP = 16
+PARK = 100
 HI_MASK = -(1 << 20)
 SIGN_BIT = -(1 << 31)
 WORD_PIECES = ((512, 512, 1024), (512, 512, 512, 512))
@@ -34,53 +35,64 @@ def tile_list_tabgate_bias_kernel(tc, tab_words, tab_scales, w, gT, b, offs, out
     nc = tc.nc
     with ExitStack() as ctx:
         keep = ctx.enter_context(tc.tile_pool(name="keep", bufs=1))
+        tables = ctx.enter_context(tc.tile_pool(name="tables", bufs=1))
         psum = ctx.enter_context(tc.psum_pool(name="psum", bufs=1))
 
         offsets = keep.tile([P, S // GROUP], U16, name="offsets")
         w_raw = [keep.tile([P, PACK, M], F32, name="w_raw%d" % a, align_bytes=64) for a in range(PASSES)]
-        scale_table = keep.tile([P, T // 4], I32, name="scale_table", tag="scale_table", align_bytes=64)
+        table_bytes = 4 * T
+        scale_table = tables.tile([P, T // 4], I32, name="scale_table", offset=table_bytes - T // 2, align_bytes=64)
         word_table = [keep.tile([P, T], I32, name="word_table%d" % a, tag="word_table%d" % a, align_bytes=64) for a in range(PASSES)]
-        gate_table = [keep.tile([P, T], F32, name="gate_table%d" % n, align_bytes=64) for n in range(N_TILES)]
+        gate_table = [tables.tile([P, T], F32, name="gate_table%d" % n, offset=n * table_bytes, align_bytes=64) for n in range(N_TILES)]
         bias = keep.tile([P, N_TILES], F32, name="bias")
+        v_scales = [keep.tile([P, S], U8, name="v_scales%d" % a, align_bytes=64) for a in range(PASSES)]
 
         def load_w(a):
             nc.sync.dma_start(out=w_raw[a][:], in_=w[a * K_PASS : (a + 1) * K_PASS, :].rearrange("(p j) n -> p j n", j=PACK))
+
+        def load_words(a):
+            nc.sync.dma_start(out=word_table[a][:], in_=tab_words[a].rearrange("p t i -> p (t i)").bitcast(I32))
 
         nc.vector.memset(scale_table[:], 0)
         nc.sync.dma_start(offsets[:], offs)
         load_w(0)
         for r in range(4):
-            for a in range(PASSES):
-                nc.sync.dma_start(out=scale_table[4 * a + r : P : 32, :], in_=tab_scales[a].rearrange("(q r) t -> r q t", r=4)[r].bitcast(I32))
+            nc.sync.dma_start(out=scale_table[r:P:32, :], in_=tab_scales[0].rearrange("(q r) t -> r q t", r=4)[r].bitcast(I32))
+        nc.sync.dma_start(out=scale_table[PARK : PARK + 16, :], in_=tab_scales[1].bitcast(I32))
         load_w(1)
         for a in range(PASSES):
-            nc.sync.dma_start(out=word_table[a][:], in_=tab_words[a].rearrange("p t i -> p (t i)").bitcast(I32))
+            load_words(a)
         with nc.allow_non_contiguous_dma(reason="one bias value a partition"):
             nc.sync.dma_start(out=bias[:], in_=b.rearrange("(c p) -> p c", p=P))
-        for n in range(N_TILES):
-            nc.sync.dma_start(out=gate_table[n][:], in_=gT[n * P : (n + 1) * P, :])
 
         identity = keep.tile([P, P], F32, name="identity", align_bytes=64)
         make_identity(nc, identity[:])
+        nc.gpsimd.memset(v_scales[1][:].bitcast(I32), 0)
 
         def bank(index, name):
             return psum.tile([P, BANK], F32, name=name, tag="bank%d" % index)
 
-        w_split = [keep.tile([P, 2, M, PACK], BF16, name="w_split%d" % a, align_bytes=64) for a in range(PASSES)]
+        w_split = []
         neg_hi = [keep.tile([P, PACK, M], I32, name="neg_hi%d" % a, align_bytes=64) for a in range(PASSES)]
 
         def picks(first, count):
             return offsets[:, first // GROUP : (first + count) // GROUP]
 
-        v_scales = keep.tile([P, S], U8, name="v_scales", align_bytes=64)
         half = S // PASSES
         for a in range(PASSES):
             nc.vector.tensor_scalar(out=neg_hi[a][:], in0=w_raw[a][:].bitcast(I32), scalar1=HI_MASK, scalar2=SIGN_BIT, op0=ALU.bitwise_and, op1=ALU.bitwise_xor)
-            nc.vector.tensor_copy(out=v_scales[:, a * half : (a + 1) * half], in_=scale_table[:].bitcast(U8).indirect(picks(a * half, half)))
+            nc.vector.tensor_copy(out=v_scales[0][:, a * half : (a + 1) * half], in_=scale_table[:].bitcast(U8).indirect(picks(a * half, half)))
+
+        for r in range(4):
+            nc.sync.dma_start(out=v_scales[1][r:P:32, :].bitcast(I32), in_=v_scales[0][PARK + r : PARK + 16 : 4, :].bitcast(I32))
+        for n in range(N_TILES):
+            nc.sync.dma_start(out=gate_table[n][:], in_=gT[n * P : (n + 1) * P, :])
+
         for a in range(PASSES):
-            lo_t = keep.tile([P, N_TILES, 2, P, 2], BF16, name="lo_t%d" % a, align_bytes=64)
+            lo_t = keep.tile([P, N_TILES, 2, P, 2], BF16, name="lo_t%d" % a, tag=("w_split1", "lo_t1")[a], align_bytes=64)
+            w_split.append(keep.tile([P, 2, M, PACK], BF16, name="w_split%d" % a, tag="w_split%d" % a, align_bytes=64))
             for n in range(N_TILES):
-                diff = bank(CHUNKS + a * N_TILES + n, "diff%d_%d" % (a, n))
+                diff = bank(((4, 5), (5, 2))[a][n], "diff%d_%d" % (a, n))
                 for j in range(PACK):
                     for first, rows in ((True, w_raw[a][:]), (False, neg_hi[a][:].bitcast(F32))):
                         nc.tensor.matmul(diff[:, j * P : (j + 1) * P], lhsT=rows[:, j, n * P : (n + 1) * P], rhs=identity[:], is_transpose=True, start=first, stop=not first)
@@ -103,7 +115,7 @@ def tile_list_tabgate_bias_kernel(tc, tab_words, tab_scales, w, gT, b, offs, out
         w_scales = [keep.tile([P, 2 * M], U8, name="w_scales%d" % a, align_bytes=64) for a in range(PASSES)]
         w_codes = []
 
-        v_words = [keep.tile([P, S], U32, name="v_words%d" % a, align_bytes=64) for a in range(PASSES)]
+        v_words = [keep.tile([P, S], U32, name="v_words%d" % a, tag=("v_words0", "w_split1")[a], align_bytes=64) for a in range(PASSES)]
         acc = [[bank(n * CHUNKS + c, "acc%d_%d" % (n, c)) for c in range(CHUNKS)] for n in range(N_TILES)]
         y = [keep.tile([P, S], F32, name="y%d" % n, align_bytes=64) for n in range(N_TILES)]
 
@@ -116,7 +128,7 @@ def tile_list_tabgate_bias_kernel(tc, tab_words, tab_scales, w, gT, b, offs, out
                     lhsT=w_codes[a][:, w_cols].bitcast(FP8X4),
                     lhsT_scale=w_scales[a][:, w_cols],
                     rhs=v_words[a][:, cols].bitcast(FP8X4),
-                    rhs_scale=v_scales[4 * a : P, cols],
+                    rhs_scale=v_scales[a][:, cols],
                     start=(a == 0 and h == 0),
                     stop=(a == PASSES - 1 and h == 1),
                 )
@@ -125,7 +137,7 @@ def tile_list_tabgate_bias_kernel(tc, tab_words, tab_scales, w, gT, b, offs, out
             nc.scalar.activation(out=y[n][:, c * BANK : (c + 1) * BANK], in_=acc[n][c][:], func=IDENTITY, bias=bias[:, n : n + 1])
 
         for a in range(PASSES):
-            codes = keep.tile([P, 2 * M], U32, name="w_codes%d" % a, tag=("scale_table", "word_table0")[a], align_bytes=64)
+            codes = keep.tile([P, 2 * M], U32, name="w_codes%d" % a, tag=("w_codes0", "word_table0")[a], align_bytes=64)
             nc.vector.quantize_mx(out=codes[:].bitcast(FP8X4), scales=w_scales[a][:], in_=w_split[a][:].rearrange("p h n j -> p (h n j)"))
             w_codes.append(codes)
             first = 0

@@ -24,11 +24,10 @@ N_TILES = M // P
 BANK = 512
 CHUNKS = S // BANK
 GROUP = 16
-PARK = 100
 HI_MASK = -(1 << 20)
 SIGN_BIT = -(1 << 31)
 WORD_PIECES = ((512, 512, 1024), (512, 512, 512, 512))
-GATE_PIECES = ((1024, 1024), (1024, 512, 384, 128))
+GATE_PIECES = ((512, 512, 1024), (1024, 512, 384, 128))
 
 
 def tile_list_tabgate_bias_kernel(tc, tab_words, tab_scales, w, gT, b, offs, out):
@@ -45,7 +44,8 @@ def tile_list_tabgate_bias_kernel(tc, tab_words, tab_scales, w, gT, b, offs, out
         word_table = [keep.tile([P, T], I32, name="word_table%d" % a, tag="word_table%d" % a, align_bytes=64) for a in range(PASSES)]
         gate_table = [tables.tile([P, T], F32, name="gate_table%d" % n, offset=n * table_bytes, align_bytes=64) for n in range(N_TILES)]
         bias = keep.tile([P, N_TILES], F32, name="bias")
-        v_scales = [keep.tile([P, S], U8, name="v_scales%d" % a, align_bytes=64) for a in range(PASSES)]
+        picked_scales = keep.tile([P, S], U8, name="picked_scales", align_bytes=64)
+        planes = [keep.tile([P, S], U8, name="planes%d" % a, align_bytes=64) for a in range(PASSES)]
 
         def load_w(a):
             nc.sync.dma_start(out=w_raw[a][:], in_=w[a * K_PASS : (a + 1) * K_PASS, :].rearrange("(p j) n -> p j n", j=PACK))
@@ -53,12 +53,11 @@ def tile_list_tabgate_bias_kernel(tc, tab_words, tab_scales, w, gT, b, offs, out
         def load_words(a):
             nc.sync.dma_start(out=word_table[a][:], in_=tab_words[a].rearrange("p t i -> p (t i)").bitcast(I32))
 
-        nc.vector.memset(scale_table[:], 0)
         nc.sync.dma_start(offsets[:], offs)
         load_w(0)
-        for r in range(4):
-            nc.sync.dma_start(out=scale_table[r:P:32, :], in_=tab_scales[0].rearrange("(q r) t -> r q t", r=4)[r].bitcast(I32))
-        nc.sync.dma_start(out=scale_table[PARK : PARK + 16, :], in_=tab_scales[1].bitcast(I32))
+        nc.sync.dma_start(out=scale_table[0:32, :], in_=tab_scales.rearrange("a q t -> (a q) t").bitcast(I32))
+        nc.vector.memset(scale_table[32:64, :], 0)
+        nc.vector.memset(scale_table[64:P, :], 0)
         load_w(1)
         for a in range(PASSES):
             load_words(a)
@@ -67,7 +66,8 @@ def tile_list_tabgate_bias_kernel(tc, tab_words, tab_scales, w, gT, b, offs, out
 
         identity = keep.tile([P, P], F32, name="identity", align_bytes=64)
         make_identity(nc, identity[:])
-        nc.gpsimd.memset(v_scales[1][:].bitcast(I32), 0)
+        for a in range(PASSES):
+            nc.gpsimd.memset(planes[a][:].bitcast(I32), 0)
 
         def bank(index, name):
             return psum.tile([P, BANK], F32, name=name, tag="bank%d" % index)
@@ -81,12 +81,17 @@ def tile_list_tabgate_bias_kernel(tc, tab_words, tab_scales, w, gT, b, offs, out
         half = S // PASSES
         for a in range(PASSES):
             nc.vector.tensor_scalar(out=neg_hi[a][:], in0=w_raw[a][:].bitcast(I32), scalar1=HI_MASK, scalar2=SIGN_BIT, op0=ALU.bitwise_and, op1=ALU.bitwise_xor)
-            nc.vector.tensor_copy(out=v_scales[0][:, a * half : (a + 1) * half], in_=scale_table[:].bitcast(U8).indirect(picks(a * half, half)))
+            nc.vector.tensor_copy(out=picked_scales[:, a * half : (a + 1) * half], in_=scale_table[:].bitcast(U8).indirect(picks(a * half, half)))
 
-        for r in range(4):
-            nc.sync.dma_start(out=v_scales[1][r:P:32, :].bitcast(I32), in_=v_scales[0][PARK + r : PARK + 16 : 4, :].bitcast(I32))
-        for n in range(N_TILES):
-            nc.sync.dma_start(out=gate_table[n][:], in_=gT[n * P : (n + 1) * P, :])
+        def place_scales(a):
+            for r in range(4):
+                nc.sync.dma_start(out=planes[a][r:P:32, :].bitcast(I32), in_=picked_scales[16 * a + r : 16 * (a + 1) : 4, :].bitcast(I32))
+
+        place_scales(0)
+        nc.sync.dma_start(out=gate_table[0][:, 0 : T // 2], in_=gT[0:P, 0 : T // 2])
+        place_scales(1)
+        nc.sync.dma_start(out=gate_table[0][:, T // 2 : T], in_=gT[0:P, T // 2 : T])
+        nc.sync.dma_start(out=gate_table[1][:], in_=gT[P : 2 * P, :])
 
         for a in range(PASSES):
             lo_t = keep.tile([P, N_TILES, 2, P, 2], BF16, name="lo_t%d" % a, tag=("w_split1", "lo_t1")[a], align_bytes=64)
@@ -116,7 +121,7 @@ def tile_list_tabgate_bias_kernel(tc, tab_words, tab_scales, w, gT, b, offs, out
         w_codes = []
 
         v_words = [keep.tile([P, S], U32, name="v_words%d" % a, tag=("v_words0", "w_split1")[a], align_bytes=64) for a in range(PASSES)]
-        acc = [[bank(n * CHUNKS + c, "acc%d_%d" % (n, c)) for c in range(CHUNKS)] for n in range(N_TILES)]
+        acc = [[bank(c, "acc0_%d" % c) for c in range(CHUNKS)], []]
         y = [keep.tile([P, S], F32, name="y%d" % n, align_bytes=64) for n in range(N_TILES)]
 
         def passes(a, n, c):
@@ -128,7 +133,7 @@ def tile_list_tabgate_bias_kernel(tc, tab_words, tab_scales, w, gT, b, offs, out
                     lhsT=w_codes[a][:, w_cols].bitcast(FP8X4),
                     lhsT_scale=w_scales[a][:, w_cols],
                     rhs=v_words[a][:, cols].bitcast(FP8X4),
-                    rhs_scale=v_scales[a][:, cols],
+                    rhs_scale=planes[a][:, cols],
                     start=(a == 0 and h == 0),
                     stop=(a == PASSES - 1 and h == 1),
                 )
@@ -149,6 +154,7 @@ def tile_list_tabgate_bias_kernel(tc, tab_words, tab_scales, w, gT, b, offs, out
                         add_bias(0, c)
                 first += count
         for c in range(CHUNKS):
+            acc[1].append(bank(c, "acc1_%d" % c))
             for a in range(PASSES):
                 passes(a, 1, c)
             add_bias(1, c)

@@ -27,7 +27,7 @@ GROUP = 16
 HI_MASK = -(1 << 20)
 SIGN_BIT = -(1 << 31)
 WORD_PIECES = ((512, 512, 1024), (512, 512, 512, 512))
-GATE_PIECES = ((512, 512, 1024), (1024, 512, 384, 128))
+GATE_PIECES = ((512, 512, 512, 512), (512, 512, 512, 384, 128))
 
 
 def tile_list_tabgate_bias_kernel(tc, tab_words, tab_scales, w, gT, b, offs, out):
@@ -96,18 +96,22 @@ def tile_list_tabgate_bias_kernel(tc, tab_words, tab_scales, w, gT, b, offs, out
         for a in range(PASSES):
             lo_t = keep.tile([P, N_TILES, 2, P, 2], BF16, name="lo_t%d" % a, tag=("w_split1", "lo_t1")[a], align_bytes=64)
             w_split.append(keep.tile([P, 2, M, PACK], BF16, name="w_split%d" % a, tag="w_split%d" % a, align_bytes=64))
+            diff = []
             for n in range(N_TILES):
-                diff = bank(((4, 5), (5, 2))[a][n], "diff%d_%d" % (a, n))
+                diff.append(bank(((4, 5), (5, 2))[a][n], "diff%d_%d" % (a, n)))
                 for j in range(PACK):
-                    for first, rows in ((True, w_raw[a][:]), (False, neg_hi[a][:].bitcast(F32))):
-                        nc.tensor.matmul(diff[:, j * P : (j + 1) * P], lhsT=rows[:, j, n * P : (n + 1) * P], rhs=identity[:], is_transpose=True, start=first, stop=not first)
-                nc.scalar.activation(out=lo_t[:, n], in_=diff[:].rearrange("n (u e p) -> n u p e", u=2, e=2), func=IDENTITY)
-            nc.scalar.activation(
-                out=w_split[a][:, 0].rearrange("p (c i) j -> p c j i", i=4),
-                in_=neg_hi[a][:].bitcast(F32).rearrange("p j (c i) -> p c j i", i=4),
-                func=IDENTITY,
-                scale=-1.0,
-            )
+                    nc.tensor.matmul(diff[n][:, j * P : (j + 1) * P], lhsT=w_raw[a][:, j, n * P : (n + 1) * P], rhs=identity[:], is_transpose=True, start=(j == 0), stop=False)
+            for n in range(N_TILES):
+                for j in range(PACK):
+                    nc.tensor.matmul(diff[n][:, j * P : (j + 1) * P], lhsT=neg_hi[a][:].bitcast(F32)[:, j, n * P : (n + 1) * P], rhs=identity[:], is_transpose=True, start=False, stop=(j == PACK - 1))
+                nc.scalar.activation(out=lo_t[:, n], in_=diff[n][:].rearrange("n (u e p) -> n u p e", u=2, e=2), func=IDENTITY)
+            for n in range(N_TILES):
+                nc.scalar.activation(
+                    out=w_split[a][:, 0, n * P : (n + 1) * P].rearrange("p (c i) j -> p c j i", i=4),
+                    in_=neg_hi[a][:].bitcast(F32)[:, :, n * P : (n + 1) * P].rearrange("p j (c i) -> p c j i", i=4),
+                    func=IDENTITY,
+                    scale=-1.0,
+                )
             back = bank(CHUNKS - PASSES + a, "back%d" % a)
             lo_words = lo_t[:].rearrange("n t u p e -> n (t u p e)").bitcast(F32)
             for block in range(N_TILES * 2):
@@ -121,15 +125,14 @@ def tile_list_tabgate_bias_kernel(tc, tab_words, tab_scales, w, gT, b, offs, out
         w_codes = []
 
         v_words = [keep.tile([P, S], U32, name="v_words%d" % a, tag=("v_words0", "w_split1")[a], align_bytes=64) for a in range(PASSES)]
-        acc = [[bank(c, "acc0_%d" % c) for c in range(CHUNKS)], []]
         y = [keep.tile([P, S], F32, name="y%d" % n, align_bytes=64) for n in range(N_TILES)]
 
-        def passes(a, n, c):
+        def passes(acc, a, n, c):
             cols = slice(c * BANK, (c + 1) * BANK)
             for h in range(2):
                 w_cols = slice(h * M + n * P, h * M + (n + 1) * P)
                 nc.tensor.matmul_mx(
-                    out=acc[n][c][:],
+                    out=acc[:],
                     lhsT=w_codes[a][:, w_cols].bitcast(FP8X4),
                     lhsT_scale=w_scales[a][:, w_cols],
                     rhs=v_words[a][:, cols].bitcast(FP8X4),
@@ -138,9 +141,6 @@ def tile_list_tabgate_bias_kernel(tc, tab_words, tab_scales, w, gT, b, offs, out
                     stop=(a == PASSES - 1 and h == 1),
                 )
 
-        def add_bias(n, c):
-            nc.scalar.activation(out=y[n][:, c * BANK : (c + 1) * BANK], in_=acc[n][c][:], func=IDENTITY, bias=bias[:, n : n + 1])
-
         for a in range(PASSES):
             codes = keep.tile([P, 2 * M], U32, name="w_codes%d" % a, tag=("w_codes0", "word_table0")[a], align_bytes=64)
             nc.vector.quantize_mx(out=codes[:].bitcast(FP8X4), scales=w_scales[a][:], in_=w_split[a][:].rearrange("p h n j -> p (h n j)"))
@@ -148,16 +148,13 @@ def tile_list_tabgate_bias_kernel(tc, tab_words, tab_scales, w, gT, b, offs, out
             first = 0
             for count in WORD_PIECES[a]:
                 nc.vector.tensor_copy(out=v_words[a][:, first : first + count], in_=word_table[a][:].bitcast(U32).indirect(picks(first, count)))
-                for c in range(first // BANK, (first + count) // BANK):
-                    passes(a, 0, c)
-                    if a == PASSES - 1:
-                        add_bias(0, c)
                 first += count
-        for c in range(CHUNKS):
-            acc[1].append(bank(c, "acc1_%d" % c))
-            for a in range(PASSES):
-                passes(a, 1, c)
-            add_bias(1, c)
+        for n in range(N_TILES):
+            for c in range(CHUNKS):
+                acc = bank(c % 2, "acc%d_%d" % (n, c))
+                for a in range(PASSES):
+                    passes(acc, a, n, c)
+                nc.scalar.activation(out=y[n][:, c * BANK : (c + 1) * BANK], in_=acc[:], func=IDENTITY, bias=bias[:, n : n + 1])
 
         for n in range(N_TILES):
             first = 0

@@ -26,8 +26,9 @@ CHUNKS = S // BANK
 GROUP = 16
 HI_MASK = -(1 << 20)
 SIGN_BIT = -(1 << 31)
-WORD_PIECES = ((512, 512, 1024), (512, 512, 512, 512))
-GATE_PIECES = ((512, 512, 512, 512), (512, 512, 512, 384, 128))
+AHEAD = 3
+EARLY = 512
+GATE_PIECES = ((512, 512, 1024), (1024, 512, 384, 128))
 
 
 def tile_list_tabgate_bias_kernel(tc, tab_words, tab_scales, w, gT, b, offs, out):
@@ -41,11 +42,11 @@ def tile_list_tabgate_bias_kernel(tc, tab_words, tab_scales, w, gT, b, offs, out
         w_raw = [keep.tile([P, PACK, M], F32, name="w_raw%d" % a, align_bytes=64) for a in range(PASSES)]
         table_bytes = 4 * T
         scale_table = tables.tile([P, T // 4], I32, name="scale_table", offset=table_bytes - T // 2, align_bytes=64)
-        word_table = [keep.tile([P, T], I32, name="word_table%d" % a, tag="word_table%d" % a, align_bytes=64) for a in range(PASSES)]
+        word_table = [keep.tile([P, T], I32, name="word_table%d" % a, align_bytes=64) for a in range(PASSES)]
         gate_table = [tables.tile([P, T], F32, name="gate_table%d" % n, offset=n * table_bytes, align_bytes=64) for n in range(N_TILES)]
         bias = keep.tile([P, N_TILES], F32, name="bias")
         picked_scales = keep.tile([P, S], U8, name="picked_scales", align_bytes=64)
-        planes = [keep.tile([P, S], U8, name="planes%d" % a, align_bytes=64) for a in range(PASSES)]
+        planes = keep.tile([P, S], U8, name="planes", align_bytes=64)
 
         def load_w(a):
             nc.sync.dma_start(out=w_raw[a][:], in_=w[a * K_PASS : (a + 1) * K_PASS, :].rearrange("(p j) n -> p j n", j=PACK))
@@ -54,65 +55,65 @@ def tile_list_tabgate_bias_kernel(tc, tab_words, tab_scales, w, gT, b, offs, out
             nc.sync.dma_start(out=word_table[a][:], in_=tab_words[a].rearrange("p t i -> p (t i)").bitcast(I32))
 
         nc.sync.dma_start(offsets[:], offs)
-        load_w(0)
-        nc.sync.dma_start(out=scale_table[0:32, :], in_=tab_scales.rearrange("a q t -> (a q) t").bitcast(I32))
-        nc.vector.memset(scale_table[32:64, :], 0)
-        nc.vector.memset(scale_table[64:P, :], 0)
-        load_w(1)
+        nc.scalar.dma_start(out=scale_table[0:32, :], in_=tab_scales.bitcast(I32).rearrange("a q t -> q a t"))
         for a in range(PASSES):
+            load_w(a)
             load_words(a)
         with nc.allow_non_contiguous_dma(reason="one bias value a partition"):
             nc.sync.dma_start(out=bias[:], in_=b.rearrange("(c p) -> p c", p=P))
+        nc.vector.memset(scale_table[32:64, :], 0)
+        nc.vector.memset(scale_table[64:P, :], 0)
+        codes_at = 2 * table_bytes
+        late_at = codes_at + 4 * 2 * M
+        hi_mask = tables.tile([P, 32], I32, name="hi_mask", offset=late_at - 64, align_bytes=64)
+        nc.gpsimd.memset(hi_mask[:], HI_MASK)
 
         identity = keep.tile([P, P], F32, name="identity", align_bytes=64)
         make_identity(nc, identity[:])
-        for a in range(PASSES):
-            nc.gpsimd.memset(planes[a][:].bitcast(I32), 0)
 
         def bank(index, name):
             return psum.tile([P, BANK], F32, name=name, tag="bank%d" % index)
 
-        w_split = []
-        neg_hi = [keep.tile([P, PACK, M], I32, name="neg_hi%d" % a, align_bytes=64) for a in range(PASSES)]
-
         def picks(first, count):
             return offsets[:, first // GROUP : (first + count) // GROUP]
 
-        half = S // PASSES
+        nc.vector.tensor_copy(out=picked_scales[:], in_=scale_table[:].bitcast(U8).indirect(offsets[:]))
+        for r in range(4):
+            nc.sync.dma_start(out=planes[r:P:4, :].bitcast(I32), in_=picked_scales[2 * r : 2 * r + 32, :].bitcast(I32))
+        for n in range(N_TILES):
+            nc.sync.dma_start(out=gate_table[n][:], in_=gT[n * P : (n + 1) * P, :])
+
+        v_words = [[] for a in range(PASSES)]
+
+        def gather_words(a, first, counts, piece):
+            v_words[a].append((first, sum(counts), piece))
+            done = 0
+            for count in counts:
+                nc.vector.tensor_copy(out=piece[:, done : done + count], in_=word_table[a][:].bitcast(U32).indirect(picks(first + done, count)))
+                done += count
+
+        neg_hi = [keep.tile([P, PACK, M], I32, name="neg_hi%d" % a, tag="neg_hi%d" % a, align_bytes=64) for a in range(PASSES)]
+        nc.vector.tensor_scalar(out=neg_hi[0][:], in0=w_raw[0][:].bitcast(I32), scalar1=HI_MASK, scalar2=SIGN_BIT, op0=ALU.bitwise_and, op1=ALU.bitwise_xor)
+        gather_words(0, 0, (EARLY,), keep.tile([P, EARLY], U32, name="v0_early", align_bytes=64))
+        for half in range(2):
+            rows = slice(2 * half, 2 * half + 2)
+            nc.vector.tensor_scalar(out=neg_hi[1][:, rows], in0=w_raw[1][:, rows].bitcast(I32), scalar1=(hi_mask[:, 0:1], HI_MASK)[half], scalar2=SIGN_BIT, op0=ALU.bitwise_and, op1=ALU.bitwise_xor)
+        gather_words(0, EARLY, (S - EARLY,), tables.tile([P, S - EARLY], U32, name="v0_late", offset=late_at, align_bytes=64))
+
+        w_split = []
         for a in range(PASSES):
-            nc.vector.tensor_scalar(out=neg_hi[a][:], in0=w_raw[a][:].bitcast(I32), scalar1=HI_MASK, scalar2=SIGN_BIT, op0=ALU.bitwise_and, op1=ALU.bitwise_xor)
-            nc.vector.tensor_copy(out=picked_scales[:, a * half : (a + 1) * half], in_=scale_table[:].bitcast(U8).indirect(picks(a * half, half)))
-
-        def place_scales(a):
-            for r in range(4):
-                nc.sync.dma_start(out=planes[a][r:P:32, :].bitcast(I32), in_=picked_scales[16 * a + r : 16 * (a + 1) : 4, :].bitcast(I32))
-
-        place_scales(0)
-        nc.sync.dma_start(out=gate_table[0][:, 0 : T // 2], in_=gT[0:P, 0 : T // 2])
-        place_scales(1)
-        nc.sync.dma_start(out=gate_table[0][:, T // 2 : T], in_=gT[0:P, T // 2 : T])
-        nc.sync.dma_start(out=gate_table[1][:], in_=gT[P : 2 * P, :])
-
-        for a in range(PASSES):
-            lo_t = keep.tile([P, N_TILES, 2, P, 2], BF16, name="lo_t%d" % a, tag=("w_split1", "lo_t1")[a], align_bytes=64)
+            lo_t = keep.tile([P, N_TILES, 2, P, 2], BF16, name="lo_t%d" % a, tag=("lo_t0", "w_split1")[a], align_bytes=64)
             w_split.append(keep.tile([P, 2, M, PACK], BF16, name="w_split%d" % a, tag="w_split%d" % a, align_bytes=64))
             diff = []
             for n in range(N_TILES):
-                diff.append(bank(((4, 5), (5, 2))[a][n], "diff%d_%d" % (a, n)))
+                diff.append(bank(4 + 2 * a + n, "diff%d_%d" % (a, n)))
                 for j in range(PACK):
                     nc.tensor.matmul(diff[n][:, j * P : (j + 1) * P], lhsT=w_raw[a][:, j, n * P : (n + 1) * P], rhs=identity[:], is_transpose=True, start=(j == 0), stop=False)
             for n in range(N_TILES):
                 for j in range(PACK):
                     nc.tensor.matmul(diff[n][:, j * P : (j + 1) * P], lhsT=neg_hi[a][:].bitcast(F32)[:, j, n * P : (n + 1) * P], rhs=identity[:], is_transpose=True, start=False, stop=(j == PACK - 1))
                 nc.scalar.activation(out=lo_t[:, n], in_=diff[n][:].rearrange("n (u e p) -> n u p e", u=2, e=2), func=IDENTITY)
-            for n in range(N_TILES):
-                nc.scalar.activation(
-                    out=w_split[a][:, 0, n * P : (n + 1) * P].rearrange("p (c i) j -> p c j i", i=4),
-                    in_=neg_hi[a][:].bitcast(F32)[:, :, n * P : (n + 1) * P].rearrange("p j (c i) -> p c j i", i=4),
-                    func=IDENTITY,
-                    scale=-1.0,
-                )
-            back = bank(CHUNKS - PASSES + a, "back%d" % a)
+            back = bank(3 + a, "back%d" % a)
             lo_words = lo_t[:].rearrange("n t u p e -> n (t u p e)").bitcast(F32)
             for block in range(N_TILES * 2):
                 nc.tensor.transpose(back[:, block * P : (block + 1) * P], lo_words[:, block * P : (block + 1) * P], identity[:])
@@ -120,41 +121,56 @@ def tile_list_tabgate_bias_kernel(tc, tab_words, tab_scales, w, gT, b, offs, out
                 out=w_split[a][:, 1].rearrange("p n j -> p (n j)").bitcast(F32).rearrange("p (t n u) -> p t n u", t=N_TILES, u=2),
                 in_=back[:].rearrange("p (t u n) -> p t n u", t=N_TILES, u=2),
             )
-
-        w_scales = [keep.tile([P, 2 * M], U8, name="w_scales%d" % a, align_bytes=64) for a in range(PASSES)]
-        w_codes = []
-
-        v_words = [keep.tile([P, S], U32, name="v_words%d" % a, tag=("v_words0", "w_split1")[a], align_bytes=64) for a in range(PASSES)]
-        y = [keep.tile([P, S], F32, name="y%d" % n, align_bytes=64) for n in range(N_TILES)]
-
-        def passes(acc, a, n, c):
-            cols = slice(c * BANK, (c + 1) * BANK)
-            for h in range(2):
-                w_cols = slice(h * M + n * P, h * M + (n + 1) * P)
-                nc.tensor.matmul_mx(
-                    out=acc[:],
-                    lhsT=w_codes[a][:, w_cols].bitcast(FP8X4),
-                    lhsT_scale=w_scales[a][:, w_cols],
-                    rhs=v_words[a][:, cols].bitcast(FP8X4),
-                    rhs_scale=planes[a][:, cols],
-                    start=(a == 0 and h == 0),
-                    stop=(a == PASSES - 1 and h == 1),
+            hi_parts = N_TILES - a
+            for part in range(hi_parts):
+                cols = slice(part * M // hi_parts, (part + 1) * M // hi_parts)
+                nc.scalar.activation(
+                    out=w_split[a][:, 0, cols].rearrange("p (c i) j -> p c j i", i=4),
+                    in_=neg_hi[a][:].bitcast(F32)[:, :, cols].rearrange("p j (c i) -> p c j i", i=4),
+                    func=IDENTITY,
+                    scale=-1.0,
                 )
 
-        for a in range(PASSES):
-            codes = keep.tile([P, 2 * M], U32, name="w_codes%d" % a, tag=("w_codes0", "word_table0")[a], align_bytes=64)
-            nc.vector.quantize_mx(out=codes[:].bitcast(FP8X4), scales=w_scales[a][:], in_=w_split[a][:].rearrange("p h n j -> p (h n j)"))
-            w_codes.append(codes)
-            first = 0
-            for count in WORD_PIECES[a]:
-                nc.vector.tensor_copy(out=v_words[a][:, first : first + count], in_=word_table[a][:].bitcast(U32).indirect(picks(first, count)))
-                first += count
+        w_scales = [keep.tile([P, 2 * M], U8, name="w_scales%d" % a, align_bytes=64) for a in range(PASSES)]
+        w_codes = [tables.tile([P, 2 * M], U32, name="w_codes0", offset=codes_at, align_bytes=64), keep.tile([P, 2 * M], U32, name="w_codes1", align_bytes=64)]
+        y = [keep.tile([P, S], F32, name="y%d" % n, align_bytes=64) for n in range(N_TILES)]
+
+        def quantize(a):
+            nc.vector.quantize_mx(out=w_codes[a][:].bitcast(FP8X4), scales=w_scales[a][:], in_=w_split[a][:].rearrange("p h n j -> p (h n j)"))
+
+        quantize(0)
+        gather_words(1, 0, (2 * BANK,), keep.tile([P, 2 * BANK], U32, name="v1_early", align_bytes=64))
+        quantize(1)
+        gather_words(1, 2 * BANK, (BANK, BANK), keep.tile([P, 2 * BANK], U32, name="v1_late", tag="neg_hi1", align_bytes=64))
+
+        def passes(acc, a, n, c):
+            runs = []
+            for first, count, piece in v_words[a]:
+                low, high = max(first, c * BANK), min(first + count, (c + 1) * BANK)
+                if low < high:
+                    runs.append((low, high, piece[:, low - first : high - first]))
+            for h in range(2):
+                w_cols = slice(h * M + n * P, h * M + (n + 1) * P)
+                for low, high, words in runs:
+                    nc.tensor.matmul_mx(
+                        out=acc[:, low - c * BANK : high - c * BANK],
+                        lhsT=w_codes[a][:, w_cols].bitcast(FP8X4),
+                        lhsT_scale=w_scales[a][:, w_cols],
+                        rhs=words.bitcast(FP8X4),
+                        rhs_scale=planes[4 * a : P, low:high],
+                        start=(a == 0 and h == 0 and low == c * BANK),
+                        stop=(a == PASSES - 1 and h == 1 and high == (c + 1) * BANK),
+                    )
+
+        acc = [[bank(n * CHUNKS + c, "acc%d_%d" % (n, c)) for c in range(CHUNKS)] for n in range(N_TILES)]
+        for c in range(AHEAD):
+            passes(acc[0][c], 0, 0, c)
         for n in range(N_TILES):
             for c in range(CHUNKS):
-                acc = bank(c % 2, "acc%d_%d" % (n, c))
                 for a in range(PASSES):
-                    passes(acc, a, n, c)
-                nc.scalar.activation(out=y[n][:, c * BANK : (c + 1) * BANK], in_=acc[:], func=IDENTITY, bias=bias[:, n : n + 1])
+                    if (n, a) != (0, 0) or c >= AHEAD:
+                        passes(acc[n][c], a, n, c)
+                nc.scalar.activation(out=y[n][:, c * BANK : (c + 1) * BANK], in_=acc[n][c][:], func=IDENTITY, bias=bias[:, n : n + 1])
 
         for n in range(N_TILES):
             first = 0

@@ -26,9 +26,8 @@ CHUNKS = S // BANK
 GROUP = 16
 HI_MASK = -(1 << 20)
 SIGN_BIT = -(1 << 31)
-AHEAD = 3
 EARLY = 512
-GATE_PIECES = ((512, 512, 1024), (1024, 512, 384, 128))
+GATE_PIECES = ((1024, 1024), (1024, 512, 384, 128))
 
 
 def tile_list_tabgate_bias_kernel(tc, tab_words, tab_scales, w, gT, b, offs, out):
@@ -39,7 +38,7 @@ def tile_list_tabgate_bias_kernel(tc, tab_words, tab_scales, w, gT, b, offs, out
         psum = ctx.enter_context(tc.psum_pool(name="psum", bufs=1))
 
         offsets = keep.tile([P, S // GROUP], U16, name="offsets")
-        w_raw = [keep.tile([P, PACK, M], F32, name="w_raw%d" % a, align_bytes=64) for a in range(PASSES)]
+        w_raw = [keep.tile([P, PACK, M], F32, name="w_raw%d" % a, tag="w_raw%d" % a, align_bytes=64) for a in range(PASSES)]
         table_bytes = 4 * T
         scale_table = tables.tile([P, T // 4], I32, name="scale_table", offset=table_bytes - T // 2, align_bytes=64)
         word_table = [keep.tile([P, T], I32, name="word_table%d" % a, align_bytes=64) for a in range(PASSES)]
@@ -63,9 +62,8 @@ def tile_list_tabgate_bias_kernel(tc, tab_words, tab_scales, w, gT, b, offs, out
             nc.sync.dma_start(out=bias[:], in_=b.rearrange("(c p) -> p c", p=P))
         nc.vector.memset(scale_table[32:64, :], 0)
         nc.vector.memset(scale_table[64:P, :], 0)
-        codes_at = 2 * table_bytes
-        late_at = codes_at + 4 * 2 * M
-        hi_mask = tables.tile([P, 32], I32, name="hi_mask", offset=late_at - 64, align_bytes=64)
+        late_at = 2 * table_bytes
+        hi_mask = tables.tile([P, 1], I32, name="hi_mask", offset=late_at, align_bytes=64)
         nc.gpsimd.memset(hi_mask[:], HI_MASK)
 
         identity = keep.tile([P, P], F32, name="identity", align_bytes=64)
@@ -132,7 +130,7 @@ def tile_list_tabgate_bias_kernel(tc, tab_words, tab_scales, w, gT, b, offs, out
                 )
 
         w_scales = [keep.tile([P, 2 * M], U8, name="w_scales%d" % a, align_bytes=64) for a in range(PASSES)]
-        w_codes = [tables.tile([P, 2 * M], U32, name="w_codes0", offset=codes_at, align_bytes=64), keep.tile([P, 2 * M], U32, name="w_codes1", align_bytes=64)]
+        w_codes = [keep.tile([P, 2 * M], U32, name="w_codes0", tag="w_raw1", align_bytes=64), keep.tile([P, 2 * M], U32, name="w_codes1", align_bytes=64)]
         y = [keep.tile([P, S], F32, name="y%d" % n, align_bytes=64) for n in range(N_TILES)]
 
         def quantize(a):
@@ -163,13 +161,10 @@ def tile_list_tabgate_bias_kernel(tc, tab_words, tab_scales, w, gT, b, offs, out
                     )
 
         acc = [[bank(n * CHUNKS + c, "acc%d_%d" % (n, c)) for c in range(CHUNKS)] for n in range(N_TILES)]
-        for c in range(AHEAD):
-            passes(acc[0][c], 0, 0, c)
-        for n in range(N_TILES):
-            for c in range(CHUNKS):
-                for a in range(PASSES):
-                    if (n, a) != (0, 0) or c >= AHEAD:
-                        passes(acc[n][c], a, n, c)
+        order = [(0, 0, 0), (0, 0, 1), (0, 0, 2), (0, 0, 3), (1, 0, 0), (1, 0, 1), (1, 0, 2), (0, 1, 0), (1, 0, 3), (1, 1, 0), (0, 1, 1), (1, 1, 1), (0, 1, 2), (1, 1, 2), (0, 1, 3), (1, 1, 3)]
+        for a, n, c in order:
+            passes(acc[n][c], a, n, c)
+            if a == PASSES - 1:
                 nc.scalar.activation(out=y[n][:, c * BANK : (c + 1) * BANK], in_=acc[n][c][:], func=IDENTITY, bias=bias[:, n : n + 1])
 
         for n in range(N_TILES):

@@ -161,7 +161,7 @@ def tile_list_tabgate_bias_kernel(tc, tab_words, tab_scales, w, gT, b, offs, out
                     )
 
         acc = [[bank(n * CHUNKS + c, "acc%d_%d" % (n, c)) for c in range(CHUNKS)] for n in range(N_TILES)]
-        order = [(0, 0, 0), (0, 0, 1), (0, 0, 2), (0, 0, 3), (1, 0, 0), (1, 0, 1), (1, 0, 2), (0, 1, 0), (1, 0, 3), (1, 1, 0), (0, 1, 1), (1, 1, 1), (0, 1, 2), (1, 1, 2), (0, 1, 3), (1, 1, 3)]
+        order = [(0, 0, 0), (0, 0, 1), (1, 0, 0), (1, 0, 1)] + [(a, n, c) for n in range(N_TILES) for c in range(CHUNKS) for a in range(PASSES) if n * CHUNKS + c >= 2]
         for a, n, c in order:
             passes(acc[n][c], a, n, c)
             if a == PASSES - 1:

@@ -15,6 +15,7 @@ U8 = mybir.dt.uint8
 FP8X4 = mybir.dt.float8_e4m3fn_x4
 ALU = mybir.AluOpType
 IDENTITY = mybir.ActivationFunctionType.Identity
+COPY = mybir.ActivationFunctionType.Copy
 
 P = 128
 PACK = 4
@@ -27,6 +28,7 @@ GROUP = 16
 HI_MASK = -(1 << 20)
 SIGN_BIT = -(1 << 31)
 EARLY = 512
+HELD = 32
 GATE_PIECES = ((1024, 1024), (1024, 512, 384, 128))
 
 
@@ -55,9 +57,10 @@ def tile_list_tabgate_bias_kernel(tc, tab_words, tab_scales, w, gT, b, offs, out
 
         nc.sync.dma_start(offsets[:], offs)
         nc.scalar.dma_start(out=scale_table[0:32, :], in_=tab_scales.bitcast(I32).rearrange("a q t -> q a t"))
-        for a in range(PASSES):
-            load_w(a)
-            load_words(a)
+        load_w(0)
+        load_words(0)
+        load_w(1)
+        load_words(1)
         with nc.allow_non_contiguous_dma(reason="one bias value a partition"):
             nc.sync.dma_start(out=bias[:], in_=b.rearrange("(c p) -> p c", p=P))
         nc.vector.memset(scale_table[32:64, :], 0)
@@ -90,56 +93,82 @@ def tile_list_tabgate_bias_kernel(tc, tab_words, tab_scales, w, gT, b, offs, out
                 nc.vector.tensor_copy(out=piece[:, done : done + count], in_=word_table[a][:].bitcast(U32).indirect(picks(first + done, count)))
                 done += count
 
-        neg_hi = [keep.tile([P, PACK, M], I32, name="neg_hi%d" % a, tag="neg_hi%d" % a, align_bytes=64) for a in range(PASSES)]
-        nc.vector.tensor_scalar(out=neg_hi[0][:], in0=w_raw[0][:].bitcast(I32), scalar1=HI_MASK, scalar2=SIGN_BIT, op0=ALU.bitwise_and, op1=ALU.bitwise_xor)
+        handed_at = late_at + 4 * S
+        neg_hi = [[keep.tile([P, PACK, P], I32, name="neg_hi%d_%d" % (a, n), tag="neg_hi%d_%d" % (a, n), align_bytes=64) if (a, n) != (0, 1) else None for n in range(N_TILES)] for a in range(PASSES)]
+        neg_hi[0][1] = tables.tile([P, PACK, P], I32, name="neg_hi_handed", offset=handed_at + 1024, align_bytes=64)
+
+        def truncate_on_scalar(a, n):
+            if a == 0:
+                neg_top = keep.tile([P, PACK, P], F32, name="neg_top%d_%d" % (a, n), align_bytes=64)
+            else:
+                neg_top = tables.tile([P, PACK, P], F32, name="neg_top%d_%d" % (a, n), offset=handed_at, align_bytes=64)
+            kept_bits = keep.tile([P, PACK, P], U32, name="kept_bits%d_%d" % (a, n), align_bytes=64)
+            halves = w_raw[a][:].bitcast(BF16)[:, :, 2 * n * P + 1 : 2 * (n + 1) * P : 2]
+            parts = (slice(0, 2), slice(2, 4)) if a == 1 else (slice(0, PACK),)
+            for rows in parts:
+                nc.scalar.activation(out=neg_top[:, rows], in_=halves[:, rows], func=COPY, scale=-1.0)
+            for rows in parts:
+                nc.scalar.activation(out=kept_bits[:, rows], in_=neg_top[:].bitcast(U32)[:, rows], func=COPY, scale=2.0**-20, bias=-15.0 / 32.0)
+            for rows in parts:
+                nc.scalar.activation(out=neg_hi[a][n][:].bitcast(U32)[:, rows], in_=kept_bits[:, rows], func=COPY, scale=2.0**20)
+
+        for n in range(N_TILES):
+            truncate_on_scalar(0, n)
         gather_words(0, 0, (EARLY,), keep.tile([P, EARLY], U32, name="v0_early", align_bytes=64))
         for half in range(2):
             rows = slice(2 * half, 2 * half + 2)
-            nc.vector.tensor_scalar(out=neg_hi[1][:, rows], in0=w_raw[1][:, rows].bitcast(I32), scalar1=(hi_mask[:, 0:1], HI_MASK)[half], scalar2=SIGN_BIT, op0=ALU.bitwise_and, op1=ALU.bitwise_xor)
+            nc.vector.tensor_scalar(out=neg_hi[1][0][:, rows], in0=w_raw[1][:, rows, 0:P].bitcast(I32), scalar1=(hi_mask[:, 0:1], HI_MASK)[half], scalar2=SIGN_BIT, op0=ALU.bitwise_and, op1=ALU.bitwise_xor)
         gather_words(0, EARLY, (S - EARLY,), tables.tile([P, S - EARLY], U32, name="v0_late", offset=late_at, align_bytes=64))
 
-        w_split = []
-        for a in range(PASSES):
-            lo_t = keep.tile([P, N_TILES, 2, P, 2], BF16, name="lo_t%d" % a, tag=("lo_t0", "w_split1")[a], align_bytes=64)
-            w_split.append(keep.tile([P, 2, M, PACK], BF16, name="w_split%d" % a, tag="w_split%d" % a, align_bytes=64))
-            diff = []
-            for n in range(N_TILES):
-                diff.append(bank(4 + 2 * a + n, "diff%d_%d" % (a, n)))
+        flat = [keep.tile([P, 2 * M * PACK], BF16, name="w_split0", align_bytes=64), tables.tile([P, 2 * M * PACK], BF16, name="w_split1", offset=handed_at + 2048, align_bytes=64)]
+        w_split = [flat[a][:].rearrange("p (s c j) -> p s c j", s=2 * N_TILES, j=PACK) for a in range(PASSES)]
+
+        def cast_high(a, n, cols):
+            nc.scalar.activation(
+                out=w_split[a][:, 2 * N_TILES - 1 - n, cols].rearrange("p (c i) j -> p c j i", i=4),
+                in_=neg_hi[a][n][:].bitcast(F32)[:, :, cols].rearrange("p j (c i) -> p c j i", i=4),
+                func=IDENTITY,
+                scale=-1.0,
+            )
+
+        def low_part(a, tiles, lo_t, diff_banks, back_bank, held):
+            diff = {n: bank(index, "diff%d_%d" % (a, n)) for index, n in zip(diff_banks, tiles)}
+            for n in tiles:
                 for j in range(PACK):
                     nc.tensor.matmul(diff[n][:, j * P : (j + 1) * P], lhsT=w_raw[a][:, j, n * P : (n + 1) * P], rhs=identity[:], is_transpose=True, start=(j == 0), stop=False)
-            for n in range(N_TILES):
+            for n in tiles:
+                cast_high(a, n, slice(held * n, P))
+            for t, n in enumerate(tiles):
                 for j in range(PACK):
-                    nc.tensor.matmul(diff[n][:, j * P : (j + 1) * P], lhsT=neg_hi[a][:].bitcast(F32)[:, j, n * P : (n + 1) * P], rhs=identity[:], is_transpose=True, start=False, stop=(j == PACK - 1))
-                nc.scalar.activation(out=lo_t[:, n], in_=diff[n][:].rearrange("n (u e p) -> n u p e", u=2, e=2), func=IDENTITY)
-            back = bank(3 + a, "back%d" % a)
-            lo_words = lo_t[:].rearrange("n t u p e -> n (t u p e)").bitcast(F32)
-            for block in range(N_TILES * 2):
-                nc.tensor.transpose(back[:, block * P : (block + 1) * P], lo_words[:, block * P : (block + 1) * P], identity[:])
+                    nc.tensor.matmul(diff[n][:, j * P : (j + 1) * P], lhsT=neg_hi[a][n][:].bitcast(F32)[:, j], rhs=identity[:], is_transpose=True, start=False, stop=(j == PACK - 1))
+                nc.scalar.activation(out=lo_t[:, t * BANK : (t + 1) * BANK].rearrange("n (u p e) -> n u p e", u=2, e=2), in_=diff[n][:].rearrange("n (u e p) -> n u p e", u=2, e=2), func=IDENTITY)
+            back = bank(back_bank, "back%d_%d" % (a, tiles[0]))
+            for block in range(2 * len(tiles)):
+                nc.tensor.transpose(back[:, block * P : (block + 1) * P], lo_t.bitcast(F32)[:, block * P : (block + 1) * P], identity[:])
             nc.scalar.copy(
-                out=w_split[a][:, 1].rearrange("p n j -> p (n j)").bitcast(F32).rearrange("p (t n u) -> p t n u", t=N_TILES, u=2),
-                in_=back[:].rearrange("p (t u n) -> p t n u", t=N_TILES, u=2),
+                out=flat[a][:].bitcast(F32).rearrange("p (s c u) -> p s c u", s=2 * N_TILES, u=2)[:, :N_TILES],
+                in_=back[:, : 2 * len(tiles) * P].rearrange("p (n u c) -> p n c u", n=len(tiles), u=2),
             )
-            hi_parts = N_TILES - a
-            for part in range(hi_parts):
-                cols = slice(part * M // hi_parts, (part + 1) * M // hi_parts)
-                nc.scalar.activation(
-                    out=w_split[a][:, 0, cols].rearrange("p (c i) j -> p c j i", i=4),
-                    in_=neg_hi[a][:].bitcast(F32)[:, :, cols].rearrange("p j (c i) -> p c j i", i=4),
-                    func=IDENTITY,
-                    scale=-1.0,
-                )
+            if held:
+                cast_high(a, tiles[-1], slice(0, held))
+
+        lo_t0 = keep.tile([P, M * PACK], BF16, name="lo_t0", align_bytes=64)
+        low_part(0, (0, 1), lo_t0[:], (4, 5), 3, 0)
+        truncate_on_scalar(1, 1)
+        low_part(1, (0, 1), flat[1][:, HELD * PACK : 2 * BANK + HELD * PACK], (6, 7), 4, HELD)
 
         w_scales = [keep.tile([P, 2 * M], U8, name="w_scales%d" % a, align_bytes=64) for a in range(PASSES)]
         w_codes = [keep.tile([P, 2 * M], U32, name="w_codes0", tag="w_raw1", align_bytes=64), keep.tile([P, 2 * M], U32, name="w_codes1", align_bytes=64)]
         y = [keep.tile([P, S], F32, name="y%d" % n, align_bytes=64) for n in range(N_TILES)]
 
         def quantize(a):
-            nc.vector.quantize_mx(out=w_codes[a][:].bitcast(FP8X4), scales=w_scales[a][:], in_=w_split[a][:].rearrange("p h n j -> p (h n j)"))
+            nc.vector.quantize_mx(out=w_codes[a][:].bitcast(FP8X4), scales=w_scales[a][:], in_=flat[a][:])
 
         quantize(0)
         gather_words(1, 0, (2 * BANK,), keep.tile([P, 2 * BANK], U32, name="v1_early", align_bytes=64))
         quantize(1)
-        gather_words(1, 2 * BANK, (BANK, BANK), keep.tile([P, 2 * BANK], U32, name="v1_late", tag="neg_hi1", align_bytes=64))
+        gather_words(1, 2 * BANK, (BANK, BANK), keep.tile([P, 2 * BANK], U32, name="v1_late", tag="neg_hi1_1", align_bytes=64))
+
 
         def passes(acc, a, n, c):
             runs = []
@@ -148,7 +177,8 @@ def tile_list_tabgate_bias_kernel(tc, tab_words, tab_scales, w, gT, b, offs, out
                 if low < high:
                     runs.append((low, high, piece[:, low - first : high - first]))
             for h in range(2):
-                w_cols = slice(h * M + n * P, h * M + (n + 1) * P)
+                slot = (2 * N_TILES - 1 - n, n)[h]
+                w_cols = slice(slot * P, (slot + 1) * P)
                 for low, high, words in runs:
                     nc.tensor.matmul_mx(
                         out=acc[:, low - c * BANK : high - c * BANK],

@@ -61,8 +61,6 @@ def tile_list_tabgate_bias_kernel(tc, tab_words, tab_scales, w, gT, b, offs, out
         load_words(0)
         load_w(1)
         load_words(1)
-        with nc.allow_non_contiguous_dma(reason="one bias value a partition"):
-            nc.sync.dma_start(out=bias[:], in_=b.rearrange("(c p) -> p c", p=P))
         nc.vector.memset(scale_table[32:64, :], 0)
         nc.vector.memset(scale_table[64:P, :], 0)
         late_at = 2 * table_bytes
@@ -81,6 +79,8 @@ def tile_list_tabgate_bias_kernel(tc, tab_words, tab_scales, w, gT, b, offs, out
         nc.vector.tensor_copy(out=picked_scales[:], in_=scale_table[:].bitcast(U8).indirect(offsets[:]))
         for r in range(4):
             nc.sync.dma_start(out=planes[r:P:4, :].bitcast(I32), in_=picked_scales[2 * r : 2 * r + 32, :].bitcast(I32))
+        with nc.allow_non_contiguous_dma(reason="one bias value a partition"):
+            nc.sync.dma_start(out=bias[:], in_=b.rearrange("(c p) -> p c", p=P))
         for n in range(N_TILES):
             nc.sync.dma_start(out=gate_table[n][:], in_=gT[n * P : (n + 1) * P, :])
 

@@ -56,13 +56,12 @@ def tile_list_tabgate_bias_kernel(tc, tab_words, tab_scales, w, gT, b, offs, out
             nc.sync.dma_start(out=word_table[a][:], in_=tab_words[a].rearrange("p t i -> p (t i)").bitcast(I32))
 
         nc.sync.dma_start(offsets[:], offs)
-        nc.scalar.dma_start(out=scale_table[0:32, :], in_=tab_scales.bitcast(I32).rearrange("a q t -> q a t"))
+        nc.vector.memset(scale_table[:], 0)
         load_w(0)
+        nc.sync.dma_start(out=scale_table[32:96:2, :], in_=tab_scales.bitcast(I32).rearrange("a q t -> q a t"))
         load_words(0)
         load_w(1)
         load_words(1)
-        nc.vector.memset(scale_table[32:64, :], 0)
-        nc.vector.memset(scale_table[64:P, :], 0)
         late_at = 2 * table_bytes
         hi_mask = tables.tile([P, 1], I32, name="hi_mask", offset=late_at, align_bytes=64)
         nc.gpsimd.memset(hi_mask[:], HI_MASK)
@@ -78,7 +77,7 @@ def tile_list_tabgate_bias_kernel(tc, tab_words, tab_scales, w, gT, b, offs, out
 
         nc.vector.tensor_copy(out=picked_scales[:], in_=scale_table[:].bitcast(U8).indirect(offsets[:]))
         for r in range(4):
-            nc.sync.dma_start(out=planes[r:P:4, :].bitcast(I32), in_=picked_scales[2 * r : 2 * r + 32, :].bitcast(I32))
+            nc.sync.dma_start(out=planes[r:P:4, :].bitcast(I32), in_=picked_scales[32 + 4 * r : 96 + 4 * r : 2, :].bitcast(I32))
         with nc.allow_non_contiguous_dma(reason="one bias value a partition"):
             nc.sync.dma_start(out=bias[:], in_=b.rearrange("(c p) -> p c", p=P))
         for n in range(N_TILES):

@@ -57,8 +57,10 @@ def tile_list_tabgate_bias_kernel(tc, tab_words, tab_scales, w, gT, b, offs, out
 
         nc.sync.dma_start(offsets[:], offs)
         nc.vector.memset(scale_table[:], 0)
-        load_w(0)
+        w_rows = w[0:K_PASS, :].rearrange("(p j) n -> p j n", j=PACK)
+        nc.sync.dma_start(out=w_raw[0][:, 0:2], in_=w_rows[:, 0:2])
         nc.sync.dma_start(out=scale_table[32:96:2, :], in_=tab_scales.bitcast(I32).rearrange("a q t -> q a t"))
+        nc.sync.dma_start(out=w_raw[0][:, 2:4], in_=w_rows[:, 2:4])
         load_words(0)
         load_w(1)
         load_words(1)

@@ -27,56 +27,63 @@ CHUNKS = S // BANK
 GROUP = 16
 HI_MASK = -(1 << 20)
 SIGN_BIT = -(1 << 31)
-EARLY = 512
-HELD = 32
-GATE_PIECES = ((1024, 1024), (1024, 512, 384, 128))
+GATE_PIECES = ((512, 512, 512, 512), (512, 512, 512, 384, 128))
+KIB = 1024
 
 
 def tile_list_tabgate_bias_kernel(tc, tab_words, tab_scales, w, gT, b, offs, out):
     nc = tc.nc
     with ExitStack() as ctx:
         keep = ctx.enter_context(tc.tile_pool(name="keep", bufs=1))
-        tables = ctx.enter_context(tc.tile_pool(name="tables", bufs=1))
+        shared = ctx.enter_context(tc.tile_pool(name="shared", bufs=1))
         psum = ctx.enter_context(tc.psum_pool(name="psum", bufs=1))
 
-        offsets = keep.tile([P, S // GROUP], U16, name="offsets")
-        w_raw = [keep.tile([P, PACK, M], F32, name="w_raw%d" % a, tag="w_raw%d" % a, align_bytes=64) for a in range(PASSES)]
-        table_bytes = 4 * T
-        scale_table = tables.tile([P, T // 4], I32, name="scale_table", offset=table_bytes - T // 2, align_bytes=64)
-        word_table = [keep.tile([P, T], I32, name="word_table%d" % a, align_bytes=64) for a in range(PASSES)]
-        gate_table = [tables.tile([P, T], F32, name="gate_table%d" % n, offset=n * table_bytes, align_bytes=64) for n in range(N_TILES)]
-        bias = keep.tile([P, N_TILES], F32, name="bias")
-        picked_scales = keep.tile([P, S], U8, name="picked_scales", align_bytes=64)
-        planes = keep.tile([P, S], U8, name="planes", align_bytes=64)
+        def tile(name, shape, dtype, at=None):
+            if at is None:
+                return keep.tile(shape, dtype, name=name, align_bytes=64)
+            return shared.tile(shape, dtype, name=name, offset=at, align_bytes=64)
 
-        def load_w(a):
-            nc.sync.dma_start(out=w_raw[a][:], in_=w[a * K_PASS : (a + 1) * K_PASS, :].rearrange("(p j) n -> p j n", j=PACK))
+        def bank(index, name):
+            return psum.tile([P, BANK], F32, name=name, tag="bank%d" % index)
+
+        codes0_at, neg_hi0_at, picked_at = 0, 1 * KIB, 9 * KIB
+        v1_late_at = picked_at + 3 * KIB // 2
+        low10_at = 19 * KIB
+
+        offsets = keep.tile([P, S // GROUP], U16, name="offsets")
+        w0_first = tile("w0_first", [P, 2, M], F32)
+        w0_second = tile("w0_second", [P, 2, M], F32)
+        w1 = tile("w1", [P, PACK, M], F32)
+        w_half = [[w0_first[:], w0_second[:]], [w1[:, 0:2], w1[:, 2:4]]]
+        scale_table = tile("scale_table", [P, T // 4], I32)
+        word_table = [tile("word_table%d" % a, [P, T], I32) for a in range(PASSES)]
+        gate_table = [tile("gate_table%d" % n, [P, T], F32) for n in range(N_TILES)]
+        bias = tile("bias", [P, N_TILES], F32)
+        picked_scales = tile("picked_scales", [P, S], U8, picked_at)
+        planes = tile("planes", [P, S], U8)
+        identity = tile("identity", [P, P], F32)
+
+        def w_rows(a):
+            return w[a * K_PASS : (a + 1) * K_PASS, :].rearrange("(p j) n -> p j n", j=PACK)
 
         def load_words(a):
             nc.sync.dma_start(out=word_table[a][:], in_=tab_words[a].rearrange("p t i -> p (t i)").bitcast(I32))
 
         nc.sync.dma_start(offsets[:], offs)
         nc.vector.memset(scale_table[:], 0)
-        w_rows = w[0:K_PASS, :].rearrange("(p j) n -> p j n", j=PACK)
-        nc.sync.dma_start(out=w_raw[0][:, 0:2], in_=w_rows[:, 0:2])
+        nc.sync.dma_start(out=w0_first[:], in_=w_rows(0)[:, 0:2])
         nc.sync.dma_start(out=scale_table[32:96:2, :], in_=tab_scales.bitcast(I32).rearrange("a q t -> q a t"))
-        nc.sync.dma_start(out=w_raw[0][:, 2:4], in_=w_rows[:, 2:4])
+        nc.sync.dma_start(out=w0_second[:], in_=w_rows(0)[:, 2:4])
         load_words(0)
-        load_w(1)
+        nc.sync.dma_start(out=w1[:], in_=w_rows(1))
         load_words(1)
-        late_at = 2 * table_bytes
-        hi_mask = tables.tile([P, 1], I32, name="hi_mask", offset=late_at, align_bytes=64)
-        nc.gpsimd.memset(hi_mask[:], HI_MASK)
-
-        identity = keep.tile([P, P], F32, name="identity", align_bytes=64)
         make_identity(nc, identity[:])
-
-        def bank(index, name):
-            return psum.tile([P, BANK], F32, name=name, tag="bank%d" % index)
 
         def picks(first, count):
             return offsets[:, first // GROUP : (first + count) // GROUP]
 
+        neg_hi0 = tile("neg_hi0", [P, PACK, M], F32, neg_hi0_at)
+        nc.vector.tensor_scalar(out=neg_hi0[:].bitcast(I32)[:, 0:2], in0=w0_first[:].bitcast(I32), scalar1=HI_MASK, scalar2=SIGN_BIT, op0=ALU.bitwise_and, op1=ALU.bitwise_xor)
         nc.vector.tensor_copy(out=picked_scales[:], in_=scale_table[:].bitcast(U8).indirect(offsets[:]))
         for r in range(4):
             nc.sync.dma_start(out=planes[r:P:4, :].bitcast(I32), in_=picked_scales[32 + 4 * r : 96 + 4 * r : 2, :].bitcast(I32))
@@ -85,123 +92,125 @@ def tile_list_tabgate_bias_kernel(tc, tab_words, tab_scales, w, gT, b, offs, out
         for n in range(N_TILES):
             nc.sync.dma_start(out=gate_table[n][:], in_=gT[n * P : (n + 1) * P, :])
 
-        v_words = [[] for a in range(PASSES)]
+        def truncate(name, pieces, top_at):
+            neg_top = [tile("neg_top%s_%d" % (name, index), list(rows.shape), F32, top_at[index]) for index, (rows, neg_hi) in enumerate(pieces)]
+            kept_bits = [tile("kept_bits%s_%d" % (name, index), list(rows.shape), U32) for index, (rows, neg_hi) in enumerate(pieces)]
+            for index, (rows, neg_hi) in enumerate(pieces):
+                nc.scalar.activation(out=neg_top[index][:], in_=rows.bitcast(BF16)[:, :, 1::2], func=COPY, scale=-1.0)
+            for index in range(len(pieces)):
+                nc.scalar.activation(out=kept_bits[index][:], in_=neg_top[index][:].bitcast(U32), func=COPY, scale=2.0**-20, bias=-15.0 / 32.0)
+            for index, (rows, neg_hi) in enumerate(pieces):
+                nc.scalar.activation(out=neg_hi.bitcast(U32), in_=kept_bits[index][:], func=COPY, scale=2.0**20)
 
-        def gather_words(a, first, counts, piece):
-            v_words[a].append((first, sum(counts), piece))
-            done = 0
-            for count in counts:
-                nc.vector.tensor_copy(out=piece[:, done : done + count], in_=word_table[a][:].bitcast(U32).indirect(picks(first + done, count)))
-                done += count
+        def turn_w(a, n, diff_bank):
+            diff = bank(diff_bank, "diff%d_%d" % (a, n))
+            for j in range(PACK):
+                nc.tensor.matmul(diff[:, j * P : (j + 1) * P], lhsT=w_half[a][j // 2][:, j % 2, n * P : (n + 1) * P], rhs=identity[:], is_transpose=True, start=(j == 0), stop=False)
+            return diff
 
-        handed_at = late_at + 4 * S
-        neg_hi = [[keep.tile([P, PACK, P], I32, name="neg_hi%d_%d" % (a, n), tag="neg_hi%d_%d" % (a, n), align_bytes=64) if (a, n) != (0, 1) else None for n in range(N_TILES)] for a in range(PASSES)]
-        neg_hi[0][1] = tables.tile([P, PACK, P], I32, name="neg_hi_handed", offset=handed_at + 1024, align_bytes=64)
+        def subtract(diff, neg_hi):
+            for j in range(PACK):
+                nc.tensor.matmul(diff[:, j * P : (j + 1) * P], lhsT=neg_hi[:, j], rhs=identity[:], is_transpose=True, start=False, stop=(j == PACK - 1))
 
-        def truncate_on_scalar(a, n):
+        def round_low(diff, low_turned):
+            nc.scalar.activation(out=low_turned.rearrange("n (u p e) -> n u p e", u=2, e=2), in_=diff[:].rearrange("n (u e p) -> n u p e", u=2, e=2), func=IDENTITY)
+
+        def cast_high(neg_hi, high):
+            nc.scalar.activation(out=high.rearrange("p (c i j) -> p c j i", i=4, j=PACK), in_=neg_hi.rearrange("p j (c i) -> p c j i", i=4), func=IDENTITY, scale=-1.0)
+
+        def turn_back(name, low_turned, low, count, back_bank):
+            back = bank(back_bank, name)
+            for block in range(2 * count):
+                nc.tensor.transpose(back[:, block * P : (block + 1) * P], low_turned.bitcast(F32)[:, block * P : (block + 1) * P], identity[:])
+            nc.scalar.copy(out=low.bitcast(F32).rearrange("p (n c u) -> p n c u", n=count, u=2), in_=back[:, : 2 * count * P].rearrange("p (n u c) -> p n c u", n=count, u=2))
+
+        w_codes, w_scales = {}, {}
+
+        def quantize(a, tiles, parts, codes_at=None):
+            width = 2 * P * len(tiles)
+            codes = tile("w_codes%d_%d" % (a, tiles[0]), [P, width], U32, codes_at)
+            scales = tile("w_scales%d_%d" % (a, tiles[0]), [P, width], U8)
+            nc.vector.quantize_mx(out=codes[:].bitcast(FP8X4), scales=scales[:], in_=parts[:])
+            for index, n in enumerate(tiles):
+                columns = [slice((len(tiles) * (1 - part) + index) * P, (len(tiles) * (1 - part) + index + 1) * P) for part in range(2)]
+                w_codes[a, n] = [codes[:, cols] for cols in columns]
+                w_scales[a, n] = [scales[:, cols] for cols in columns]
+
+        v_words = {}
+
+        def gather_words(a, first, count, at=None):
+            piece = tile("v%d_%d" % (a, first), [P, count], U32, at)
+            nc.vector.tensor_copy(out=piece[:], in_=word_table[a][:].bitcast(U32).indirect(picks(first, count)))
+            for c in range(first // BANK, (first + count) // BANK):
+                v_words[a, c] = piece[:, c * BANK - first : (c + 1) * BANK - first]
+
+        y = [tile("y%d" % n, [P, S], F32) for n in range(N_TILES)]
+
+        acc = {}
+        acc_bank = ((3, 4, 2, 1), (5, 6, 7, 0))
+
+        def passes(a, n, c):
             if a == 0:
-                neg_top = keep.tile([P, PACK, P], F32, name="neg_top%d_%d" % (a, n), align_bytes=64)
-            else:
-                neg_top = tables.tile([P, PACK, P], F32, name="neg_top%d_%d" % (a, n), offset=handed_at, align_bytes=64)
-            kept_bits = keep.tile([P, PACK, P], U32, name="kept_bits%d_%d" % (a, n), align_bytes=64)
-            halves = w_raw[a][:].bitcast(BF16)[:, :, 2 * n * P + 1 : 2 * (n + 1) * P : 2]
-            parts = (slice(0, 2), slice(2, 4)) if a == 1 else (slice(0, PACK),)
-            for rows in parts:
-                nc.scalar.activation(out=neg_top[:, rows], in_=halves[:, rows], func=COPY, scale=-1.0)
-            for rows in parts:
-                nc.scalar.activation(out=kept_bits[:, rows], in_=neg_top[:].bitcast(U32)[:, rows], func=COPY, scale=2.0**-20, bias=-15.0 / 32.0)
-            for rows in parts:
-                nc.scalar.activation(out=neg_hi[a][n][:].bitcast(U32)[:, rows], in_=kept_bits[:, rows], func=COPY, scale=2.0**20)
-
-        for n in range(N_TILES):
-            truncate_on_scalar(0, n)
-        gather_words(0, 0, (EARLY,), keep.tile([P, EARLY], U32, name="v0_early", align_bytes=64))
-        for half in range(2):
-            rows = slice(2 * half, 2 * half + 2)
-            nc.vector.tensor_scalar(out=neg_hi[1][0][:, rows], in0=w_raw[1][:, rows, 0:P].bitcast(I32), scalar1=(hi_mask[:, 0:1], HI_MASK)[half], scalar2=SIGN_BIT, op0=ALU.bitwise_and, op1=ALU.bitwise_xor)
-        gather_words(0, EARLY, (S - EARLY,), tables.tile([P, S - EARLY], U32, name="v0_late", offset=late_at, align_bytes=64))
-
-        flat = [keep.tile([P, 2 * M * PACK], BF16, name="w_split0", align_bytes=64), tables.tile([P, 2 * M * PACK], BF16, name="w_split1", offset=handed_at + 2048, align_bytes=64)]
-        w_split = [flat[a][:].rearrange("p (s c j) -> p s c j", s=2 * N_TILES, j=PACK) for a in range(PASSES)]
-
-        def cast_high(a, n, cols):
-            nc.scalar.activation(
-                out=w_split[a][:, 2 * N_TILES - 1 - n, cols].rearrange("p (c i) j -> p c j i", i=4),
-                in_=neg_hi[a][n][:].bitcast(F32)[:, :, cols].rearrange("p j (c i) -> p c j i", i=4),
-                func=IDENTITY,
-                scale=-1.0,
-            )
-
-        def low_part(a, tiles, lo_t, diff_banks, back_bank, held):
-            diff = {n: bank(index, "diff%d_%d" % (a, n)) for index, n in zip(diff_banks, tiles)}
-            for n in tiles:
-                for j in range(PACK):
-                    nc.tensor.matmul(diff[n][:, j * P : (j + 1) * P], lhsT=w_raw[a][:, j, n * P : (n + 1) * P], rhs=identity[:], is_transpose=True, start=(j == 0), stop=False)
-            for n in tiles:
-                cast_high(a, n, slice(held * n, P))
-            for t, n in enumerate(tiles):
-                for j in range(PACK):
-                    nc.tensor.matmul(diff[n][:, j * P : (j + 1) * P], lhsT=neg_hi[a][n][:].bitcast(F32)[:, j], rhs=identity[:], is_transpose=True, start=False, stop=(j == PACK - 1))
-                nc.scalar.activation(out=lo_t[:, t * BANK : (t + 1) * BANK].rearrange("n (u p e) -> n u p e", u=2, e=2), in_=diff[n][:].rearrange("n (u e p) -> n u p e", u=2, e=2), func=IDENTITY)
-            back = bank(back_bank, "back%d_%d" % (a, tiles[0]))
-            for block in range(2 * len(tiles)):
-                nc.tensor.transpose(back[:, block * P : (block + 1) * P], lo_t.bitcast(F32)[:, block * P : (block + 1) * P], identity[:])
-            nc.scalar.copy(
-                out=flat[a][:].bitcast(F32).rearrange("p (s c u) -> p s c u", s=2 * N_TILES, u=2)[:, :N_TILES],
-                in_=back[:, : 2 * len(tiles) * P].rearrange("p (n u c) -> p n c u", n=len(tiles), u=2),
-            )
-            if held:
-                cast_high(a, tiles[-1], slice(0, held))
-
-        lo_t0 = keep.tile([P, M * PACK], BF16, name="lo_t0", align_bytes=64)
-        low_part(0, (0, 1), lo_t0[:], (4, 5), 3, 0)
-        truncate_on_scalar(1, 1)
-        low_part(1, (0, 1), flat[1][:, HELD * PACK : 2 * BANK + HELD * PACK], (6, 7), 4, HELD)
-
-        w_scales = [keep.tile([P, 2 * M], U8, name="w_scales%d" % a, align_bytes=64) for a in range(PASSES)]
-        w_codes = [keep.tile([P, 2 * M], U32, name="w_codes0", tag="w_raw1", align_bytes=64), keep.tile([P, 2 * M], U32, name="w_codes1", align_bytes=64)]
-        y = [keep.tile([P, S], F32, name="y%d" % n, align_bytes=64) for n in range(N_TILES)]
-
-        def quantize(a):
-            nc.vector.quantize_mx(out=w_codes[a][:].bitcast(FP8X4), scales=w_scales[a][:], in_=flat[a][:])
-
-        quantize(0)
-        gather_words(1, 0, (2 * BANK,), keep.tile([P, 2 * BANK], U32, name="v1_early", align_bytes=64))
-        quantize(1)
-        gather_words(1, 2 * BANK, (BANK, BANK), keep.tile([P, 2 * BANK], U32, name="v1_late", tag="neg_hi1_1", align_bytes=64))
-
-
-        def passes(acc, a, n, c):
-            runs = []
-            for first, count, piece in v_words[a]:
-                low, high = max(first, c * BANK), min(first + count, (c + 1) * BANK)
-                if low < high:
-                    runs.append((low, high, piece[:, low - first : high - first]))
+                acc[n, c] = bank(acc_bank[n][c], "acc%d_%d" % (n, c))
             for h in range(2):
-                slot = (2 * N_TILES - 1 - n, n)[h]
-                w_cols = slice(slot * P, (slot + 1) * P)
-                for low, high, words in runs:
-                    nc.tensor.matmul_mx(
-                        out=acc[:, low - c * BANK : high - c * BANK],
-                        lhsT=w_codes[a][:, w_cols].bitcast(FP8X4),
-                        lhsT_scale=w_scales[a][:, w_cols],
-                        rhs=words.bitcast(FP8X4),
-                        rhs_scale=planes[4 * a : P, low:high],
-                        start=(a == 0 and h == 0 and low == c * BANK),
-                        stop=(a == PASSES - 1 and h == 1 and high == (c + 1) * BANK),
-                    )
-
-        acc = [[bank(n * CHUNKS + c, "acc%d_%d" % (n, c)) for c in range(CHUNKS)] for n in range(N_TILES)]
-        order = [(0, 0, 0), (0, 0, 1), (1, 0, 0), (1, 0, 1)] + [(a, n, c) for n in range(N_TILES) for c in range(CHUNKS) for a in range(PASSES) if n * CHUNKS + c >= 2]
-        for a, n, c in order:
-            passes(acc[n][c], a, n, c)
+                nc.tensor.matmul_mx(
+                    out=acc[n, c][:],
+                    lhsT=w_codes[a, n][h].bitcast(FP8X4),
+                    lhsT_scale=w_scales[a, n][h],
+                    rhs=v_words[a, c].bitcast(FP8X4),
+                    rhs_scale=planes[4 * a : P, c * BANK : (c + 1) * BANK],
+                    start=(a == 0 and h == 0),
+                    stop=(a == PASSES - 1 and h == 1),
+                )
             if a == PASSES - 1:
-                nc.scalar.activation(out=y[n][:, c * BANK : (c + 1) * BANK], in_=acc[n][c][:], func=IDENTITY, bias=bias[:, n : n + 1])
+                nc.scalar.activation(out=y[n][:, c * BANK : (c + 1) * BANK], in_=acc[n, c][:], func=IDENTITY, bias=bias[:, n : n + 1])
+
+        parts0 = tile("parts0", [P, 4 * BANK], BF16)
+        low_turned0 = tile("low_turned0", [P, 2 * BANK], BF16)
+        diff0 = [turn_w(0, n, 2 * n) for n in range(N_TILES)]
+        truncate("0", [(w0_second[:, :, n * P : (n + 1) * P], neg_hi0[:, 2:4, n * P : (n + 1) * P]) for n in range(N_TILES)], (None, None))
+        for n in range(N_TILES):
+            subtract(diff0[n], neg_hi0[:, :, n * P : (n + 1) * P])
+            round_low(diff0[n], low_turned0[:, n * BANK : (n + 1) * BANK])
+        for n in range(N_TILES):
+            cast_high(neg_hi0[:, :, n * P : (n + 1) * P], parts0[:, (2 + n) * BANK : (3 + n) * BANK])
+        turn_back("back0", low_turned0[:], parts0[:, 0 : 2 * BANK], 2, 1)
+        gather_words(0, 0, S)
+
+        neg_hi1 = tile("neg_hi1", [P, PACK, M], F32)
+        parts10 = tile("parts10", [P, 2 * BANK], BF16)
+        parts11 = tile("parts11", [P, 2 * BANK], BF16, low10_at + KIB // 2)
+        low_turned10 = tile("low_turned10", [P, BANK], BF16, low10_at)
+        low_turned11 = tile("low_turned11", [P, BANK], BF16, picked_at + KIB // 2)
+        diff1 = [turn_w(1, n, 2 * n) for n in range(N_TILES)]
+        truncate("1", [(w1[:, :, n * P : (n + 1) * P], neg_hi1[:, :, n * P : (n + 1) * P]) for n in range(N_TILES)], (neg_hi0_at + 2 * KIB, neg_hi0_at))
+        for n in range(N_TILES):
+            subtract(diff1[n], neg_hi1[:, :, n * P : (n + 1) * P])
+        round_low(diff1[0], low_turned10[:])
+        cast_high(neg_hi1[:, :, 0:P], parts10[:, BANK : 2 * BANK])
+        turn_back("back10", low_turned10[:], parts10[:, 0:BANK], 1, 1)
+        round_low(diff1[1], low_turned11[:])
+        cast_high(neg_hi1[:, :, P:M], parts11[:, BANK : 2 * BANK])
+        quantize(0, (0, 1), parts0, codes_at=codes0_at)
+        gather_words(1, 0, S // 2)
+        quantize(1, (0,), parts10, codes_at=picked_at - KIB // 2)
+        gather_words(1, S // 2, S // 2, v1_late_at)
+        for c in range(2):
+            passes(0, 0, c)
+        turn_back("back11", low_turned11[:], parts11[:, 0:BANK], 1, 1)
+        quantize(1, (1,), parts11)
+        for c in range(2):
+            passes(1, 0, c)
+        for n in range(N_TILES):
+            for c in range(CHUNKS):
+                if n * CHUNKS + c >= 2:
+                    for a in range(PASSES):
+                        passes(a, n, c)
 
         for n in range(N_TILES):
             first = 0
             for count in GATE_PIECES[n]:
-                gated = keep.tile([P, count], F32, name="gated%d_%d" % (n, first), align_bytes=64)
+                gated = tile("gated%d_%d" % (n, first), [P, count], F32)
                 nc.vector.tensor_tensor(out=gated[:], in0=gate_table[n][:].indirect(picks(first, count)), in1=y[n][:, first : first + count], op=ALU.mult)
                 nc.sync.dma_start(out=out[n * P : (n + 1) * P, first : first + count], in_=gated[:])
                 first += count

@@ -27,7 +27,7 @@ CHUNKS = S // BANK
 GROUP = 16
 HI_MASK = -(1 << 20)
 SIGN_BIT = -(1 << 31)
-GATE_PIECES = ((512, 512, 512, 512), (512, 512, 512, 384, 128))
+GATE_PIECES = ((512, 512, 512, 512), (512, 512, 640, 256, 128))
 KIB = 1024
 
 
@@ -181,26 +181,25 @@ def tile_list_tabgate_bias_kernel(tc, tab_words, tab_scales, w, gT, b, offs, out
         parts10 = tile("parts10", [P, 2 * BANK], BF16)
         parts11 = tile("parts11", [P, 2 * BANK], BF16, low10_at + KIB // 2)
         low_turned10 = tile("low_turned10", [P, BANK], BF16, low10_at)
-        low_turned11 = tile("low_turned11", [P, BANK], BF16, picked_at + KIB // 2)
+        low_turned11 = tile("low_turned11", [P, BANK], BF16)
         diff1 = [turn_w(1, n, 2 * n) for n in range(N_TILES)]
         truncate("1", [(w1[:, :, n * P : (n + 1) * P], neg_hi1[:, :, n * P : (n + 1) * P]) for n in range(N_TILES)], (neg_hi0_at + 2 * KIB, neg_hi0_at))
         for n in range(N_TILES):
             subtract(diff1[n], neg_hi1[:, :, n * P : (n + 1) * P])
         round_low(diff1[0], low_turned10[:])
+        round_low(diff1[1], low_turned11[:])
         cast_high(neg_hi1[:, :, 0:P], parts10[:, BANK : 2 * BANK])
         turn_back("back10", low_turned10[:], parts10[:, 0:BANK], 1, 1)
-        round_low(diff1[1], low_turned11[:])
         cast_high(neg_hi1[:, :, P:M], parts11[:, BANK : 2 * BANK])
+        turn_back("back11", low_turned11[:], parts11[:, 0:BANK], 1, 0)
         quantize(0, (0, 1), parts0, codes_at=codes0_at)
         gather_words(1, 0, S // 2)
         quantize(1, (0,), parts10, codes_at=picked_at - KIB // 2)
         gather_words(1, S // 2, S // 2, v1_late_at)
-        for c in range(2):
-            passes(0, 0, c)
-        turn_back("back11", low_turned11[:], parts11[:, 0:BANK], 1, 1)
-        quantize(1, (1,), parts11)
-        for c in range(2):
-            passes(1, 0, c)
+        quantize(1, (1,), parts11, codes_at=picked_at + KIB // 2)
+        for a in range(PASSES):
+            for c in range(2):
+                passes(a, 0, c)
         for n in range(N_TILES):
             for c in range(CHUNKS):
                 if n * CHUNKS + c >= 2:

@@ -59,6 +59,7 @@ def tile_list_tabgate_bias_kernel(tc, tab_words, tab_scales, w, gT, b, offs, out
         word_table = [tile("word_table%d" % a, [P, T], I32) for a in range(PASSES)]
         gate_table = [tile("gate_table%d" % n, [P, T], F32) for n in range(N_TILES)]
         bias = tile("bias", [P, N_TILES], F32)
+        bias_rows = tile("bias_rows", [P, P], F32)
         picked_scales = tile("picked_scales", [P, S], U8, picked_at)
         planes = tile("planes", [P, S], U8)
         identity = tile("identity", [P, P], F32)
@@ -71,12 +72,14 @@ def tile_list_tabgate_bias_kernel(tc, tab_words, tab_scales, w, gT, b, offs, out
 
         nc.sync.dma_start(offsets[:], offs)
         nc.vector.memset(scale_table[:], 0)
+        nc.vector.memset(bias_rows[:], 0.0)
         nc.sync.dma_start(out=w0_first[:], in_=w_rows(0)[:, 0:2])
         nc.sync.dma_start(out=scale_table[32:96:2, :], in_=tab_scales.bitcast(I32).rearrange("a q t -> q a t"))
         nc.sync.dma_start(out=w0_second[:], in_=w_rows(0)[:, 2:4])
         load_words(0)
         nc.sync.dma_start(out=w1[:], in_=w_rows(1))
         load_words(1)
+        nc.sync.dma_start(out=bias_rows[0:N_TILES, :], in_=b.rearrange("(c p) -> c p", p=P))
         make_identity(nc, identity[:])
 
         def picks(first, count):
@@ -87,8 +90,6 @@ def tile_list_tabgate_bias_kernel(tc, tab_words, tab_scales, w, gT, b, offs, out
         nc.vector.tensor_copy(out=picked_scales[:], in_=scale_table[:].bitcast(U8).indirect(offsets[:]))
         for r in range(4):
             nc.sync.dma_start(out=planes[r:P:4, :].bitcast(I32), in_=picked_scales[32 + 4 * r : 96 + 4 * r : 2, :].bitcast(I32))
-        with nc.allow_non_contiguous_dma(reason="one bias value a partition"):
-            nc.sync.dma_start(out=bias[:], in_=b.rearrange("(c p) -> p c", p=P))
         for n in range(N_TILES):
             nc.sync.dma_start(out=gate_table[n][:], in_=gT[n * P : (n + 1) * P, :])
 
@@ -192,6 +193,9 @@ def tile_list_tabgate_bias_kernel(tc, tab_words, tab_scales, w, gT, b, offs, out
         turn_back("back10", low_turned10[:], parts10[:, 0:BANK], 1, 1)
         cast_high(neg_hi1[:, :, P:M], parts11[:, BANK : 2 * BANK])
         turn_back("back11", low_turned11[:], parts11[:, 0:BANK], 1, 0)
+        bias_turned = bank(5, "bias_turned")
+        nc.tensor.transpose(bias_turned[:, 0:P], bias_rows[:], identity[:])
+        nc.scalar.copy(out=bias[:], in_=bias_turned[:, 0:N_TILES])
         quantize(0, (0, 1), parts0, codes_at=codes0_at)
         gather_words(1, 0, S // 2)
         quantize(1, (0,), parts10, codes_at=picked_at - KIB // 2)

from contextlib import ExitStack

import concourse.mybir as mybir
from concourse.masks import make_identity

K, M, T, S = 1024, 256, 4096, 2048
FLOPS = 2 * 2 * K * M * S

F32 = mybir.dt.float32
BF16 = mybir.dt.bfloat16
I32 = mybir.dt.int32
U32 = mybir.dt.uint32
U16 = mybir.dt.uint16
U8 = mybir.dt.uint8
FP8X4 = mybir.dt.float8_e4m3fn_x4
ALU = mybir.AluOpType
IDENTITY = mybir.ActivationFunctionType.Identity
COPY = mybir.ActivationFunctionType.Copy

P = 128
PACK = 4
K_PASS = P * PACK
PASSES = K // K_PASS
N_TILES = M // P
BANK = 512
CHUNKS = S // BANK
GROUP = 16
HI_MASK = -(1 << 20)
SIGN_BIT = -(1 << 31)
GATE_PIECES = ((512, 512, 512, 512), (512, 512, 640, 256, 128))
KIB = 1024


def tile_list_tabgate_bias_kernel(tc, tab_words, tab_scales, w, gT, b, offs, out):
    nc = tc.nc
    with ExitStack() as ctx:
        keep = ctx.enter_context(tc.tile_pool(name="keep", bufs=1))
        shared = ctx.enter_context(tc.tile_pool(name="shared", bufs=1))
        psum = ctx.enter_context(tc.psum_pool(name="psum", bufs=1))

        def tile(name, shape, dtype, at=None):
            if at is None:
                return keep.tile(shape, dtype, name=name, align_bytes=64)
            return shared.tile(shape, dtype, name=name, offset=at, align_bytes=64)

        def bank(index, name):
            return psum.tile([P, BANK], F32, name=name, tag="bank%d" % index)

        codes0_at, neg_hi0_at, picked_at = 0, 1 * KIB, 9 * KIB
        v1_late_at = picked_at + 3 * KIB // 2
        low10_at = 19 * KIB

        offsets = keep.tile([P, S // GROUP], U16, name="offsets")
        w0_first = tile("w0_first", [P, 2, M], F32)
        w0_second = tile("w0_second", [P, 2, M], F32)
        w1 = tile("w1", [P, PACK, M], F32)
        w_half = [[w0_first[:], w0_second[:]], [w1[:, 0:2], w1[:, 2:4]]]
        scale_table = tile("scale_table", [P, T // 4], I32)
        word_table = [tile("word_table%d" % a, [P, T], I32) for a in range(PASSES)]
        gate_table = [tile("gate_table%d" % n, [P, T], F32) for n in range(N_TILES)]
        bias = tile("bias", [P, N_TILES], F32)
        bias_rows = tile("bias_rows", [P, P], F32)
        picked_scales = tile("picked_scales", [P, S], U8, picked_at)
        planes = tile("planes", [P, S], U8)
        identity = tile("identity", [P, P], F32)

        def w_rows(a):
            return w[a * K_PASS : (a + 1) * K_PASS, :].rearrange("(p j) n -> p j n", j=PACK)

        def load_words(a):
            nc.sync.dma_start(out=word_table[a][:], in_=tab_words[a].rearrange("p t i -> p (t i)").bitcast(I32))

        nc.sync.dma_start(offsets[:], offs)
        nc.vector.memset(scale_table[:], 0)
        nc.vector.memset(bias_rows[:], 0.0)
        nc.sync.dma_start(out=w0_first[:], in_=w_rows(0)[:, 0:2])
        nc.sync.dma_start(out=scale_table[32:96:2, :], in_=tab_scales.bitcast(I32).rearrange("a q t -> q a t"))
        nc.sync.dma_start(out=w0_second[:], in_=w_rows(0)[:, 2:4])
        load_words(0)
        nc.sync.dma_start(out=w1[:], in_=w_rows(1))
        load_words(1)
        nc.sync.dma_start(out=bias_rows[0:N_TILES, :], in_=b.rearrange("(c p) -> c p", p=P))
        make_identity(nc, identity[:])

        def picks(first, count):
            return offsets[:, first // GROUP : (first + count) // GROUP]

        neg_hi0 = tile("neg_hi0", [P, PACK, M], F32, neg_hi0_at)
        nc.vector.tensor_scalar(out=neg_hi0[:].bitcast(I32)[:, 0:2], in0=w0_first[:].bitcast(I32), scalar1=HI_MASK, scalar2=SIGN_BIT, op0=ALU.bitwise_and, op1=ALU.bitwise_xor)
        nc.vector.tensor_copy(out=picked_scales[:], in_=scale_table[:].bitcast(U8).indirect(offsets[:]))
        for r in range(4):
            nc.sync.dma_start(out=planes[r:P:4, :].bitcast(I32), in_=picked_scales[32 + 4 * r : 96 + 4 * r : 2, :].bitcast(I32))
        for n in range(N_TILES):
            nc.sync.dma_start(out=gate_table[n][:], in_=gT[n * P : (n + 1) * P, :])

        def truncate(name, pieces, top_at):
            neg_top = [tile("neg_top%s_%d" % (name, index), list(rows.shape), F32, top_at[index]) for index, (rows, neg_hi) in enumerate(pieces)]
            kept_bits = [tile("kept_bits%s_%d" % (name, index), list(rows.shape), U32) for index, (rows, neg_hi) in enumerate(pieces)]
            for index, (rows, neg_hi) in enumerate(pieces):
                nc.scalar.activation(out=neg_top[index][:], in_=rows.bitcast(BF16)[:, :, 1::2], func=COPY, scale=-1.0)
            for index in range(len(pieces)):
                nc.scalar.activation(out=kept_bits[index][:], in_=neg_top[index][:].bitcast(U32), func=COPY, scale=2.0**-20, bias=-15.0 / 32.0)
            for index, (rows, neg_hi) in enumerate(pieces):
                nc.scalar.activation(out=neg_hi.bitcast(U32), in_=kept_bits[index][:], func=COPY, scale=2.0**20)

        def turn_w(a, n, diff_bank):
            diff = bank(diff_bank, "diff%d_%d" % (a, n))
            for j in range(PACK):
                nc.tensor.matmul(diff[:, j * P : (j + 1) * P], lhsT=w_half[a][j // 2][:, j % 2, n * P : (n + 1) * P], rhs=identity[:], is_transpose=True, start=(j == 0), stop=False)
            return diff

        def subtract(diff, neg_hi):
            for j in range(PACK):
                nc.tensor.matmul(diff[:, j * P : (j + 1) * P], lhsT=neg_hi[:, j], rhs=identity[:], is_transpose=True, start=False, stop=(j == PACK - 1))

        def round_low(diff, low_turned):
            nc.scalar.activation(out=low_turned.rearrange("n (u p e) -> n u p e", u=2, e=2), in_=diff[:].rearrange("n (u e p) -> n u p e", u=2, e=2), func=IDENTITY)

        def cast_high(neg_hi, high):
            nc.scalar.activation(out=high.rearrange("p (c i j) -> p c j i", i=4, j=PACK), in_=neg_hi.rearrange("p j (c i) -> p c j i", i=4), func=IDENTITY, scale=-1.0)

        def turn_back(name, low_turned, low, count, back_bank):
            back = bank(back_bank, name)
            for block in range(2 * count):
                nc.tensor.transpose(back[:, block * P : (block + 1) * P], low_turned.bitcast(F32)[:, block * P : (block + 1) * P], identity[:])
            nc.scalar.copy(out=low.bitcast(F32).rearrange("p (n c u) -> p n c u", n=count, u=2), in_=back[:, : 2 * count * P].rearrange("p (n u c) -> p n c u", n=count, u=2))

        w_codes, w_scales = {}, {}

        def quantize(a, tiles, parts, codes_at=None):
            width = 2 * P * len(tiles)
            codes = tile("w_codes%d_%d" % (a, tiles[0]), [P, width], U32, codes_at)
            scales = tile("w_scales%d_%d" % (a, tiles[0]), [P, width], U8)
            nc.vector.quantize_mx(out=codes[:].bitcast(FP8X4), scales=scales[:], in_=parts[:])
            for index, n in enumerate(tiles):
                columns = [slice((len(tiles) * (1 - part) + index) * P, (len(tiles) * (1 - part) + index + 1) * P) for part in range(2)]
                w_codes[a, n] = [codes[:, cols] for cols in columns]
                w_scales[a, n] = [scales[:, cols] for cols in columns]

        v_words = {}

        def gather_words(a, first, count, at=None):
            piece = tile("v%d_%d" % (a, first), [P, count], U32, at)
            nc.vector.tensor_copy(out=piece[:], in_=word_table[a][:].bitcast(U32).indirect(picks(first, count)))
            for c in range(first // BANK, (first + count) // BANK):
                v_words[a, c] = piece[:, c * BANK - first : (c + 1) * BANK - first]

        y = [tile("y%d" % n, [P, S], F32) for n in range(N_TILES)]

        acc = {}
        acc_bank = ((3, 4, 2, 1), (5, 6, 7, 0))

        def passes(a, n, c):
            if a == 0:
                acc[n, c] = bank(acc_bank[n][c], "acc%d_%d" % (n, c))
            for h in range(2):
                nc.tensor.matmul_mx(
                    out=acc[n, c][:],
                    lhsT=w_codes[a, n][h].bitcast(FP8X4),
                    lhsT_scale=w_scales[a, n][h],
                    rhs=v_words[a, c].bitcast(FP8X4),
                    rhs_scale=planes[4 * a : P, c * BANK : (c + 1) * BANK],
                    start=(a == 0 and h == 0),
                    stop=(a == PASSES - 1 and h == 1),
                )
            if a == PASSES - 1:
                nc.scalar.activation(out=y[n][:, c * BANK : (c + 1) * BANK], in_=acc[n, c][:], func=IDENTITY, bias=bias[:, n : n + 1])

        parts0 = tile("parts0", [P, 4 * BANK], BF16)
        low_turned0 = tile("low_turned0", [P, 2 * BANK], BF16)
        diff0 = [turn_w(0, n, 2 * n) for n in range(N_TILES)]
        truncate("0", [(w0_second[:, :, n * P : (n + 1) * P], neg_hi0[:, 2:4, n * P : (n + 1) * P]) for n in range(N_TILES)], (None, None))
        for n in range(N_TILES):
            subtract(diff0[n], neg_hi0[:, :, n * P : (n + 1) * P])
            round_low(diff0[n], low_turned0[:, n * BANK : (n + 1) * BANK])
        for n in range(N_TILES):
            cast_high(neg_hi0[:, :, n * P : (n + 1) * P], parts0[:, (2 + n) * BANK : (3 + n) * BANK])
        turn_back("back0", low_turned0[:], parts0[:, 0 : 2 * BANK], 2, 1)
        gather_words(0, 0, S)

        neg_hi1 = tile("neg_hi1", [P, PACK, M], F32)
        parts10 = tile("parts10", [P, 2 * BANK], BF16)
        parts11 = tile("parts11", [P, 2 * BANK], BF16, low10_at + KIB // 2)
        low_turned10 = tile("low_turned10", [P, BANK], BF16, low10_at)
        low_turned11 = tile("low_turned11", [P, BANK], BF16)
        diff1 = [turn_w(1, n, 2 * n) for n in range(N_TILES)]
        truncate("1", [(w1[:, :, n * P : (n + 1) * P], neg_hi1[:, :, n * P : (n + 1) * P]) for n in range(N_TILES)], (neg_hi0_at + 2 * KIB, neg_hi0_at))
        for n in range(N_TILES):
            subtract(diff1[n], neg_hi1[:, :, n * P : (n + 1) * P])
        round_low(diff1[0], low_turned10[:])
        round_low(diff1[1], low_turned11[:])
        cast_high(neg_hi1[:, :, 0:P], parts10[:, BANK : 2 * BANK])
        turn_back("back10", low_turned10[:], parts10[:, 0:BANK], 1, 1)
        cast_high(neg_hi1[:, :, P:M], parts11[:, BANK : 2 * BANK])
        turn_back("back11", low_turned11[:], parts11[:, 0:BANK], 1, 0)
        bias_turned = bank(5, "bias_turned")
        nc.tensor.transpose(bias_turned[:, 0:P], bias_rows[:], identity[:])
        nc.scalar.copy(out=bias[:], in_=bias_turned[:, 0:N_TILES])
        quantize(0, (0, 1), parts0, codes_at=codes0_at)
        gather_words(1, 0, S // 2)
        quantize(1, (0,), parts10, codes_at=picked_at - KIB // 2)
        gather_words(1, S // 2, S // 2, v1_late_at)
        quantize(1, (1,), parts11, codes_at=picked_at + KIB // 2)
        for a in range(PASSES):
            for c in range(2):
                passes(a, 0, c)
        for n in range(N_TILES):
            for c in range(CHUNKS):
                if n * CHUNKS + c >= 2:
                    for a in range(PASSES):
                        passes(a, n, c)

        for n in range(N_TILES):
            first = 0
            for count in GATE_PIECES[n]:
                gated = tile("gated%d_%d" % (n, first), [P, count], F32)
                nc.vector.tensor_tensor(out=gated[:], in0=gate_table[n][:].indirect(picks(first, count)), in1=y[n][:, first : first + count], op=ALU.mult)
                nc.sync.dma_start(out=out[n * P : (n + 1) * P, first : first + count], in_=gated[:])
                first += count
